import numpy as np
import ml_dtypes


def mxq(x, axis, fmt="e4m3"):
    dtype, down = {"e4m3": (ml_dtypes.float8_e4m3fn, 7), "e5m2": (ml_dtypes.float8_e5m2, 14)}[fmt]
    v = np.moveaxis(np.asarray(x, np.float32).astype(ml_dtypes.bfloat16).astype(np.float64), axis, -1)
    blocks = v.reshape(v.shape[:-1] + (-1, 32))
    amax = np.abs(blocks).max(-1, keepdims=True)
    byte = np.maximum(np.where(amax > 0, np.frexp(amax)[1] - 1 + 127, 0) - down, 1)
    scale = np.exp2(byte - 127.0)
    codes = (blocks / scale).astype(np.float32).astype(dtype).astype(np.float64)
    return np.moveaxis((codes * scale).reshape(v.shape), -1, axis)


WIDE = False


def mx_kscale(k):
    if not WIDE:
        return np.ones(k)
    levels = np.array([30, -30])
    if k % 512:
        return np.exp2(np.random.permutation(np.resize(levels, k // 32))).repeat(32)
    a = np.empty((k // 512, 16))
    for p in range(k // 512):
        a[p, :8] = np.random.permutation(np.resize(levels, 8))
        for g in range(8):
            far = levels[np.abs(levels - a[p, g]) >= 10]
            a[p, g + 8] = far[np.random.randint(len(far))]
    return np.exp2(a.ravel()).repeat(32)


BF16 = ml_dtypes.bfloat16


def bf(x):
    return np.asarray(x, np.float32).astype(BF16)


def f64(x):
    return np.asarray(x).astype(np.float64)


E2M1 = np.array([0.0, 0.5, 1.0, 1.5, 2.0, 3.0, 4.0, 6.0, -0.0, -0.5, -1.0, -1.5, -2.0, -3.0, -4.0, -6.0])


def pack_weight(w, fmt):
    k, n = w.shape
    w = f64(bf(w)).reshape(k // 32, 32, n)
    amax = np.abs(w).max(1)
    if fmt in ("e4m3", "e5m2"):
        byte = np.frexp(amax)[1] - 1 + 127 - (7 if fmt == "e4m3" else 14)
    else:
        mant, ex = np.frexp(amax / 6.0)
        byte = np.where(mant > 0.5, ex, ex - 1) + 127
    byte = np.clip(np.where(amax > 0, byte, 1), 1, 254)
    scaled = (w * np.exp2(127.0 - byte)[:, None, :]).reshape(k, n).astype(np.float32)
    by_word = np.ascontiguousarray(scaled.reshape(k // 512, 128, 4, n).transpose(0, 1, 3, 2))
    if fmt in ("e4m3", "e5m2"):
        words = by_word.astype(ml_dtypes.float8_e4m3fn if fmt == "e4m3" else ml_dtypes.float8_e5m2).view(np.uint8)
    else:
        c = by_word.astype(ml_dtypes.float4_e2m1fn).view(np.uint8) & 0xF
        words = c[..., 0::2] | (c[..., 1::2] << 4)
    return np.ascontiguousarray(words), np.ascontiguousarray(byte.astype(np.uint8).reshape(k // 512, 16, n))


def unpack_weight(words, scales, fmt):
    g, p, n, _ = words.shape
    if fmt in ("e4m3", "e5m2"):
        vals = np.ascontiguousarray(words).view(ml_dtypes.float8_e4m3fn if fmt == "e4m3" else ml_dtypes.float8_e5m2).astype(np.float64)
    else:
        nib = np.empty((g, p, n, 4), np.uint8)
        nib[..., 0::2] = words & 0xF
        nib[..., 1::2] = words >> 4
        vals = E2M1[nib]
    vals = vals * np.repeat(np.exp2(scales.astype(np.float64) - 127.0), 8, axis=1)[..., None]
    return vals.transpose(0, 1, 3, 2).reshape(g * 512, n)

def planes(Y):
    n, m = Y.shape
    b = f64(bf(Y)).reshape(n // 32, 32, m)
    amax = np.abs(b).max(1)
    byte = np.clip(np.where(amax > 0, np.frexp(amax)[1] - 1 + 127 - 7, 1), 1, 254)
    codes = (b * np.exp2(127.0 - byte)[:, None, :]).reshape(n, m).astype(np.float32).astype(ml_dtypes.float8_e4m3fn).view(np.uint8)
    words = codes.reshape(n // 512, 128, 4, m).transpose(0, 1, 3, 2)
    return np.ascontiguousarray(words), np.ascontiguousarray(byte.astype(np.uint8).reshape(n // 512, 16, m))


EVEN, ODD, RHS = 1536, 1536, 1024


def setup_inputs():
    s = mx_kscale(ODD)
    size = np.exp(0.8 * np.random.randn(EVEN))
    chi = np.random.randn(ODD, RHS) * np.exp(np.random.randn(ODD, RHS))
    chi_words, chi_scales = pack_weight(chi / s[:, None], "e5m2")
    d_eo = 2.0 / np.sqrt(ODD) * size[:, None] * np.random.randn(EVEN, ODD)
    return {
        "d_eo": bf(d_eo * s[None, :]),
        "chi_words": chi_words,
        "chi_scales": chi_scales,
        "phi": bf(size[:, None] * np.random.randn(EVEN, RHS)),
        "kappa": bf(0.35 * np.exp(0.15 * np.random.randn(RHS))),
    }


def reference(d_eo, chi_words, chi_scales, phi, kappa):
    chi = unpack_weight(chi_words, chi_scales, "e5m2")
    d = mxq(f64(d_eo), 1, "e4m3")
    hop = d @ chi
    y = f64(phi) - np.square(f64(kappa))[None, :] * hop
    Y = y.reshape(EVEN, RHS)
    words, scales = planes(Y)
    return y, words, scales

@@ -1,0 +1,281 @@
+from contextlib import ExitStack
+
+import concourse.mybir as mybir
+from concourse.masks import make_identity
+
+EVEN, ODD, RHS = 1536, 1536, 1024
+FLOPS = 2 * EVEN * ODD * RHS
+
+F32 = mybir.dt.float32
+BF16 = mybir.dt.bfloat16
+I32 = mybir.dt.int32
+U32 = mybir.dt.uint32
+U8 = mybir.dt.uint8
+E4M3X4 = mybir.dt.float8_e4m3fn_x4
+E5M2X4 = mybir.dt.float8_e5m2_x4
+ALU = mybir.AluOpType
+
+P = 128
+PACK = 4
+SPAN = P * PACK
+GROUPS = EVEN // SPAN
+PASSES = ODD // SPAN
+N = 512
+HALVES = RHS // N
+CHUNKS = GROUPS * HALVES
+SLOTS = CHUNKS * PACK
+
+
+def tile_schur_closing_hop_k2_kernel(tc, d_eo, chi_words, chi_scales, phi, kappa, out_0, out_1, out_2):
+    nc = tc.nc
+    with ExitStack() as ctx:
+        keep = ctx.enter_context(tc.tile_pool(name="keep", bufs=1))
+        stage = ctx.enter_context(tc.tile_pool(name="stage", bufs=4))
+        turn_ps = ctx.enter_context(tc.psum_pool(name="turn_ps", bufs=3))
+        hop_ps = ctx.enter_context(tc.psum_pool(name="hop_ps", bufs=5))
+        ctx.enter_context(tc.manual_schedule())
+
+        ident = keep.tile([P, P], F32, name="ident")
+        make_identity(nc, ident[:])
+
+        chi_plane = keep.tile([P, PASSES * RHS], U8, name="chi_plane", align_bytes=64)
+        nc.vector.memset(chi_plane[:].bitcast(I32), 0)
+
+        d_rows = {}
+        phi_sb = {}
+        chi_sb = {}
+
+        def load_d(g, t0, t1):
+            raw = keep.tile([P, t1 - t0, ODD], BF16, name="d_raw_%d_%d" % (g, t0))
+            src = d_eo[g * SPAN:(g + 1) * SPAN, :].rearrange("(p t) k -> p t k", t=PACK)
+            nc.sync.dma_start(out=raw[:], in_=src[:, t0:t1, :])
+            for t in range(t0, t1):
+                d_rows[(g, t)] = raw[:, t - t0, :].bitcast(F32)
+
+        def load_phi(g, h0, h1, t0, t1):
+            raw = keep.tile([P, t1 - t0, (h1 - h0) * N], BF16, name="phi_%d_%d_%d" % (g, h0, t0))
+            src = phi[g * SPAN:(g + 1) * SPAN, h0 * N:h1 * N].rearrange("(p t) r -> p t r", t=PACK)
+            nc.sync.dma_start(out=raw[:], in_=src[:, t0:t1, :])
+            for h in range(h0, h1):
+                for t in range(t0, t1, 2):
+                    phi_sb[(g, h, t // 2)] = raw[:, t - t0:t - t0 + 2, (h - h0) * N:(h - h0 + 1) * N]
+
+        def load_chi(h, c0, c1):
+            raw = keep.tile([P, c1 - c0, N], U32, name="chi_%d_%d" % (h, c0), align_bytes=64)
+            src = chi_words.rearrange("c p n t -> p c (n t)")[:, c0:c1, h * N * PACK:(h + 1) * N * PACK]
+            nc.sync.dma_start(out=raw[:].bitcast(I32), in_=src.bitcast(I32))
+            for c in range(c0, c1):
+                chi_sb[(h, c)] = raw[:, c - c0, :]
+
+        kappa_sb = keep.tile([P, RHS // P], BF16, name="kappa_sb")
+
+        load_d(0, 0, 1)
+        load_d(0, 1, 2)
+        nc.sync.dma_start(out=kappa_sb[:], in_=kappa.rearrange("(p m) -> p m", p=P))
+        for q in range(4):
+            nc.sync.dma_start(
+                out=chi_plane[32 * q:32 * q + 4, :].rearrange("p (c n) -> p c n", c=PASSES).bitcast(I32),
+                in_=chi_scales[:, 4 * q:4 * q + 4, :].rearrange("c q n -> q c n").bitcast(I32),
+            )
+        load_chi(0, 0, 1)
+        load_chi(0, 1, 3)
+        load_d(0, 2, 3)
+        load_phi(0, 0, 1, 0, 2)
+        load_d(0, 3, 4)
+        load_phi(0, 0, 1, 2, 4)
+        load_chi(1, 0, 3)
+        load_phi(0, 1, 2, 0, 2)
+        load_d(1, 0, 2)
+        load_phi(0, 1, 2, 2, 4)
+        load_d(1, 2, 4)
+        load_phi(1, 0, 2, 0, 4)
+        load_d(2, 0, 2)
+        load_d(2, 2, 4)
+        load_phi(2, 0, 2, 0, 4)
+
+        d_turned = {}
+        d_codes = {}
+        d_scales = {}
+
+        def batches(g, t0, t1):
+            units = [(g, t, c) for t in range(t0, t1) for c in range(PASSES)]
+            return [tuple(units[i:i + 2]) for i in range(0, len(units), 2)]
+
+        def turn(batch):
+            bank = turn_ps.tile([P, 2, 2, P], F32, name="turn_bank")
+            for i, (g, t, c) in enumerate(batch):
+                for u in range(2):
+                    nc.tensor.transpose(bank[:, i, u, :], d_rows[(g, t)][:, 256 * c + u:256 * (c + 1):2], ident[:])
+            grouped = stage.tile([P, 2 * SPAN], BF16, name="d_grouped", align_bytes=64)
+            nb = len(batch)
+            nc.scalar.copy(
+                out=grouped[:, :nb * SPAN].bitcast(F32).rearrange("p (i r u) -> p i r u", i=nb, u=2),
+                in_=bank[:, :nb, :, :].rearrange("p i u r -> p i r u"),
+            )
+            d_turned[batch] = grouped[:, :nb * SPAN]
+
+        def quantize_d(batch):
+            nb = len(batch)
+            name = "%d_%d_%d" % batch[0]
+            codes = keep.tile([P, nb * P], U32, name="d_codes_" + name, align_bytes=64)
+            scales = keep.tile([P, nb * P], U8, name="d_scales_" + name, align_bytes=64)
+            nc.vector.quantize_mx(out=codes[:].bitcast(E4M3X4), scales=scales[:], in_=d_turned[batch])
+            for i, unit in enumerate(batch):
+                d_codes[unit] = codes[:, i * P:(i + 1) * P]
+                d_scales[unit] = scales[:, i * P:(i + 1) * P]
+
+        y_f32 = [keep.tile([P, PACK, N], F32, name="y_f32_%d" % j) for j in range(CHUNKS)]
+        y_bf16 = [keep.tile([P, N, PACK], BF16, name="y_bf16_%d" % j, align_bytes=64) for j in range(CHUNKS)]
+        y_codes = [keep.tile([P, N], U32, name="y_codes_%d" % j, align_bytes=64) for j in range(CHUNKS)]
+        y_plane = keep.tile([P, GROUPS, RHS], U8, name="y_plane", align_bytes=64)
+        kappa2 = keep.tile([P, P, RHS // P], F32, name="kappa2")
+        kappa2_row = kappa2[:].rearrange("p j m -> p (j m)")
+        hop = {}
+
+        def multiply(s):
+            j, t = divmod(s, PACK)
+            g, h = divmod(j, HALVES)
+            bank = hop_ps.tile([P, N], F32, name="hop_bank")
+            for c in range(PASSES):
+                nc.tensor.matmul_mx(
+                    out=bank[:],
+                    lhsT=d_codes[(g, t, c)].bitcast(E4M3X4),
+                    lhsT_scale=d_scales[(g, t, c)],
+                    rhs=chi_sb[(h, c)].bitcast(E5M2X4),
+                    rhs_scale=chi_plane[:, c * RHS + h * N:c * RHS + (h + 1) * N],
+                    start=(c == 0),
+                    stop=(c == PASSES - 1),
+                )
+            hop[s] = bank
+
+        def scale(s, n0=0, n1=N):
+            j, t = divmod(s, PACK)
+            h = j % HALVES
+            nc.vector.tensor_tensor(
+                out=y_f32[j][:, t, n0:n1], in0=hop[s][:, n0:n1], in1=kappa2_row[:, h * N + n0:h * N + n1], op=ALU.mult
+            )
+
+        def subtract(j, t0, t1, n0=0, n1=N):
+            g, h = divmod(j, HALVES)
+            part = y_f32[j][:, t0:t1, n0:n1]
+            src = phi_sb[(g, h, t0 // 2)][:, t0 % 2:t0 % 2 + t1 - t0, n0:n1]
+            nc.vector.tensor_tensor(out=part, in0=src, in1=part, op=ALU.subtract)
+
+        def weave_views(j, n0, n1):
+            dst = y_bf16[j][:, n0:n1, :].rearrange("p (c i) t -> p c t i", i=4)
+            src = y_f32[j][:, :, n0:n1].rearrange("p t (c i) -> p c t i", i=4)
+            return dst, src
+
+        def weave(j, n0, n1):
+            dst, src = weave_views(j, n0, n1)
+            nc.scalar.copy(out=dst, in_=src)
+
+        def quantize_y(j, n0, n1):
+            g, h = divmod(j, HALVES)
+            nc.vector.quantize_mx(
+                out=y_codes[j][:, n0:n1].bitcast(E4M3X4),
+                scales=y_plane[:, g, h * N + n0:h * N + n1],
+                in_=y_bf16[j][:, n0:n1, :].rearrange("p n t -> p (n t)"),
+            )
+
+        def store_y(j, t0, t1, n0=0, n1=N):
+            g, h = divmod(j, HALVES)
+            dst = out_0[g * SPAN:(g + 1) * SPAN, h * N + n0:h * N + n1].rearrange("(p t) r -> p t r", t=PACK)
+            nc.sync.dma_start(out=dst[:, t0:t1, :], in_=y_f32[j][:, t0:t1, n0:n1])
+
+        def store_codes(j):
+            g, h = divmod(j, HALVES)
+            dst = out_1[g].rearrange("p n t -> p (n t)")[:, h * N * PACK:(h + 1) * N * PACK]
+            nc.sync.dma_start(out=dst.bitcast(I32), in_=y_codes[j][:].bitcast(I32))
+
+        def store_plane(g0, g1, queues):
+            for q in range(4):
+                queues[q % len(queues)].dma_start(
+                    out=out_2[g0:g1, 4 * q:4 * q + 4, :].rearrange("g q n -> q g n").bitcast(I32),
+                    in_=y_plane[32 * q:32 * q + 4, g0:g1, :].bitcast(I32),
+                )
+
+        kappa2_col = keep.tile([P, RHS // P], F32, name="kappa2_col")
+        nc.vector.tensor_tensor(out=kappa2_col[:], in0=kappa_sb[:], in1=kappa_sb[:], op=ALU.mult)
+        first = [batches(0, t, t + 1) for t in range(PACK)]
+        for b in first[0] + first[1]:
+            turn(b)
+        for m0 in range(0, RHS // P, 4):
+            bank = hop_ps.tile([P, N], F32, name="hop_bank")
+            for m in range(4):
+                nc.tensor.transpose(
+                    bank[:, m * P:(m + 1) * P], kappa2_col[:, m0 + m:m0 + m + 1].to_broadcast([P, P]), ident[:]
+                )
+            nc.scalar.copy(out=kappa2[:, :, m0:m0 + 4], in_=bank[:].rearrange("p (m j) -> p j m", m=4))
+        for b in first[0] + first[1]:
+            quantize_d(b)
+        multiply(0)
+        multiply(1)
+        scale(0)
+        scale(1)
+        subtract(0, 0, 1)
+        for b in first[2]:
+            turn(b)
+            quantize_d(b)
+        subtract(0, 1, 2)
+        for b in first[3]:
+            turn(b)
+            quantize_d(b)
+
+        half = N // 2
+        pending = []
+        for s in range(2, SLOTS - 2):
+            j, t = divmod(s, PACK)
+            g = j // HALVES
+            multiply(s)
+            scale(s)
+            if s % 2 == 0 and s >= 4:
+                jj, tt = divmod(s - 2, PACK)
+                subtract(jj, tt, tt + 2)
+                if tt == 2:
+                    store_y(jj, 0, PACK)
+                    weave(jj, 0, half)
+                for b in pending[:2]:
+                    quantize_d(b)
+                pending = pending[2:]
+            if s % 2 == 1:
+                for b in pending:
+                    quantize_d(b)
+                pending = []
+                if s % 8 in (5, 7) and g + 1 < GROUPS:
+                    pending = batches(g + 1, s % 8 - 5, s % 8 - 3)
+                    for b in pending:
+                        turn(b)
+                if t == 1 and j >= 1:
+                    weave(j - 1, half, N)
+                if t == 3 and j >= 1:
+                    quantize_y(j - 1, 0, half)
+                if t == 1 and j >= 2:
+                    quantize_y(j - 2, half, N)
+                    store_codes(j - 2)
+                    if j - 2 == 2 * HALVES - 1:
+                        store_plane(0, 2, [nc.sync])
+
+        last = CHUNKS - 1
+        multiply(SLOTS - 2)
+        multiply(SLOTS - 1)
+        scale(SLOTS - 2, 0, half)
+        subtract(last, 0, 2)
+        store_y(last, 0, 2)
+        scale(SLOTS - 1, 0, half)
+        scale(SLOTS - 2, half, N)
+        subtract(last, 2, 4, 0, half)
+        weave(last, 0, half)
+        store_y(last, 2, 4, 0, half)
+        scale(SLOTS - 1, half, N)
+        quantize_y(last - 1, 0, half)
+        subtract(last, 2, 4, half, N)
+        store_y(last, 2, 4, half, N)
+        quantize_y(last - 1, half, N)
+        store_codes(last - 1)
+        dst, src = weave_views(last, half, N)
+        nc.vector.tensor_copy(out=dst, in_=src)
+        quantize_y(last, 0, half)
+        quantize_y(last, half, N)
+        store_codes(last)
+        store_plane(2, 3, [nc.scalar, nc.sync])

@@ -26,24 +26,60 @@ CHUNKS = GROUPS * HALVES
 SLOTS = CHUNKS * PACK
 
 
+TURN_BANKS = 3
+HOP_BANKS = 5
+
+
 def tile_schur_closing_hop_k2_kernel(tc, d_eo, chi_words, chi_scales, phi, kappa, out_0, out_1, out_2):
     nc = tc.nc
+    vector, scalar, gpsimd = nc.vector, nc.scalar, nc.gpsimd
     with ExitStack() as ctx:
         keep = ctx.enter_context(tc.tile_pool(name="keep", bufs=1))
-        stage = ctx.enter_context(tc.tile_pool(name="stage", bufs=4))
-        turn_ps = ctx.enter_context(tc.psum_pool(name="turn_ps", bufs=3))
-        hop_ps = ctx.enter_context(tc.psum_pool(name="hop_ps", bufs=5))
+        psum = ctx.enter_context(tc.psum_pool(name="psum", bufs=1))
         ctx.enter_context(tc.manual_schedule())
+
+        turn_count = []
+        hop_count = []
+
+        def turn_tile():
+            turn_count.append(0)
+            return psum.tile([P, 2, 2, P], F32, name="turn_bank_%d" % ((len(turn_count) - 1) % TURN_BANKS))
+
+        def hop_tile():
+            hop_count.append(0)
+            return psum.tile([P, N], F32, name="hop_bank_%d" % ((len(hop_count) - 1) % HOP_BANKS))
 
         ident = keep.tile([P, P], F32, name="ident")
         make_identity(nc, ident[:])
 
+        zeros = keep.tile([P, PACK * N], BF16, name="zeros", align_bytes=64)
+        nc.vector.memset(zeros[:].bitcast(I32), 0)
         chi_plane = keep.tile([P, PASSES * RHS], U8, name="chi_plane", align_bytes=64)
         nc.vector.memset(chi_plane[:].bitcast(I32), 0)
+        warm_codes = keep.tile([P, N + P], U32, name="warm_codes", align_bytes=64)
+        warm_scales = keep.tile([P, N + P], U8, name="warm_scales", align_bytes=64)
+        nc.vector.quantize_mx(out=warm_codes[:, :N].bitcast(E5M2X4), scales=warm_scales[:, :N], in_=zeros[:])
+        nc.vector.quantize_mx(out=warm_codes[:, N:].bitcast(E4M3X4), scales=warm_scales[:, N:], in_=zeros[:, :SPAN])
+        warm_bank = hop_tile()
+
+        def warm():
+            nc.tensor.matmul_mx(
+                out=warm_bank[:],
+                lhsT=warm_codes[:, N:].bitcast(E4M3X4),
+                lhsT_scale=warm_scales[:, N:],
+                rhs=warm_codes[:, :N].bitcast(E5M2X4),
+                rhs_scale=warm_scales[:, :N],
+                start=True,
+                stop=True,
+            )
 
         d_rows = {}
         phi_sb = {}
         chi_sb = {}
+        kappa_sb = keep.tile([P, RHS // P], BF16, name="kappa_sb")
+        kappa2_col = keep.tile([P, RHS // P], F32, name="kappa2_col")
+        kappa2_row = keep.tile([P, RHS], F32, name="kappa2_row")
+        kappa2_bank = {}
 
         def load_d(g, t0, t1):
             raw = keep.tile([P, t1 - t0, ODD], BF16, name="d_raw_%d_%d" % (g, t0))
@@ -52,13 +88,12 @@ def tile_schur_closing_hop_k2_kernel(tc, d_eo, chi_words, chi_scales, phi, kappa
             for t in range(t0, t1):
                 d_rows[(g, t)] = raw[:, t - t0, :].bitcast(F32)
 
-        def load_phi(g, h0, h1, t0, t1):
-            raw = keep.tile([P, t1 - t0, (h1 - h0) * N], BF16, name="phi_%d_%d_%d" % (g, h0, t0))
-            src = phi[g * SPAN:(g + 1) * SPAN, h0 * N:h1 * N].rearrange("(p t) r -> p t r", t=PACK)
-            nc.sync.dma_start(out=raw[:], in_=src[:, t0:t1, :])
-            for h in range(h0, h1):
-                for t in range(t0, t1, 2):
-                    phi_sb[(g, h, t // 2)] = raw[:, t - t0:t - t0 + 2, (h - h0) * N:(h - h0 + 1) * N]
+        def load_phi(g, pair):
+            raw = keep.tile([P, 2, RHS], BF16, name="phi_%d_%d" % (g, pair))
+            src = phi[g * SPAN:(g + 1) * SPAN, :].rearrange("(p t) r -> p t r", t=PACK)
+            nc.sync.dma_start(out=raw[:], in_=src[:, 2 * pair:2 * pair + 2, :])
+            for i in range(2):
+                phi_sb[(g, 2 * pair + i)] = raw[:, i, :]
 
         def load_chi(h, c0, c1):
             raw = keep.tile([P, c1 - c0, N], U32, name="chi_%d_%d" % (h, c0), align_bytes=64)
@@ -67,75 +102,108 @@ def tile_schur_closing_hop_k2_kernel(tc, d_eo, chi_words, chi_scales, phi, kappa
             for c in range(c0, c1):
                 chi_sb[(h, c)] = raw[:, c - c0, :]
 
-        kappa_sb = keep.tile([P, RHS // P], BF16, name="kappa_sb")
+        def load_kappa():
+            nc.sync.dma_start(
+                out=kappa_sb[:].rearrange("p (h m) -> p h m", m=PACK),
+                in_=kappa.rearrange("(h p m) -> p h m", p=P, m=PACK),
+            )
 
-        load_d(0, 0, 1)
-        load_d(0, 1, 2)
-        nc.sync.dma_start(out=kappa_sb[:], in_=kappa.rearrange("(p m) -> p m", p=P))
-        for q in range(4):
+        def load_chi_scales(q):
             nc.sync.dma_start(
                 out=chi_plane[32 * q:32 * q + 4, :].rearrange("p (c n) -> p c n", c=PASSES).bitcast(I32),
                 in_=chi_scales[:, 4 * q:4 * q + 4, :].rearrange("c q n -> q c n").bitcast(I32),
             )
-        load_chi(0, 0, 1)
-        load_chi(0, 1, 3)
-        load_d(0, 2, 3)
-        load_phi(0, 0, 1, 0, 2)
-        load_d(0, 3, 4)
-        load_phi(0, 0, 1, 2, 4)
-        load_chi(1, 0, 3)
-        load_phi(0, 1, 2, 0, 2)
-        load_d(1, 0, 2)
-        load_phi(0, 1, 2, 2, 4)
-        load_d(1, 2, 4)
-        load_phi(1, 0, 2, 0, 4)
-        load_d(2, 0, 2)
-        load_d(2, 2, 4)
-        load_phi(2, 0, 2, 0, 4)
 
+        def square_kappa():
+            nc.vector.tensor_tensor(out=kappa2_col[:], in0=kappa_sb[:], in1=kappa_sb[:], op=ALU.mult)
+
+        def spread_kappa2(h):
+            bank = hop_tile()
+            for m in range(PACK):
+                column = kappa2_col[:, h * PACK + m:h * PACK + m + 1]
+                nc.tensor.transpose(bank[:, m * P:(m + 1) * P], column.to_broadcast([P, P]), ident[:])
+            kappa2_bank[h] = bank
+
+        def copy_kappa2(h):
+            nc.scalar.copy(
+                out=kappa2_row[:, h * N:(h + 1) * N].rearrange("p (j m) -> p j m", m=PACK),
+                in_=kappa2_bank[h][:].rearrange("p (m j) -> p j m", m=PACK),
+            )
+
+        units = [[(g, t, c) for t in range(PACK) for c in range(PASSES)] for g in range(GROUPS)]
+        work = [[tuple(row[i:i + 2]) for i in range(0, len(row), 2)] for row in units]
+        work[0] = [tuple(units[0][3 * t + a:3 * t + b]) for t in range(PACK) for a, b in ((0, 2), (2, 3))]
+        d_split = {}
+        d_bank = {}
         d_turned = {}
         d_codes = {}
         d_scales = {}
 
-        def batches(g, t0, t1):
-            units = [(g, t, c) for t in range(t0, t1) for c in range(PASSES)]
-            return [tuple(units[i:i + 2]) for i in range(0, len(units), 2)]
+        def copy_on(engine, out, in_):
+            if engine is scalar:
+                nc.scalar.copy(out=out, in_=in_)
+            else:
+                nc.vector.tensor_copy(out=out, in_=in_)
+
+        def split_words(engine, batch):
+            g, t, c = batch[0]
+            nb = len(batch)
+            split = keep.tile([P, nb, 2, P], F32, name="d_split", bufs=5)
+            if batch[-1][1] == t:
+                src = d_rows[(g, t)][:, 256 * c:256 * (c + nb)]
+                copy_on(engine, split[:], src.rearrange("p (i r u) -> p i u r", i=nb, u=2))
+            else:
+                for i, (g, t, c) in enumerate(batch):
+                    src = d_rows[(g, t)][:, 256 * c:256 * (c + 1)]
+                    copy_on(engine, split[:, i, :, :], src.rearrange("p (r u) -> p u r", u=2))
+            d_split[batch] = split
 
         def turn(batch):
-            bank = turn_ps.tile([P, 2, 2, P], F32, name="turn_bank")
+            bank = turn_tile()
             for i, (g, t, c) in enumerate(batch):
                 for u in range(2):
-                    nc.tensor.transpose(bank[:, i, u, :], d_rows[(g, t)][:, 256 * c + u:256 * (c + 1):2], ident[:])
-            grouped = stage.tile([P, 2 * SPAN], BF16, name="d_grouped", align_bytes=64)
+                    if batch in d_split:
+                        words = d_split[batch][:, i, u, :]
+                    else:
+                        words = d_rows[(g, t)][:, 256 * c + u:256 * (c + 1):2]
+                    nc.tensor.transpose(bank[:, i, u, :], words, ident[:])
+            d_bank[batch] = bank
+
+        def gather(batch):
             nb = len(batch)
+            grouped = keep.tile([P, nb * SPAN], BF16, name="d_grouped", bufs=7, align_bytes=64)
             nc.scalar.copy(
-                out=grouped[:, :nb * SPAN].bitcast(F32).rearrange("p (i r u) -> p i r u", i=nb, u=2),
-                in_=bank[:, :nb, :, :].rearrange("p i u r -> p i r u"),
+                out=grouped[:].bitcast(F32).rearrange("p (i r u) -> p i r u", i=nb, u=2),
+                in_=d_bank[batch][:, :nb, :, :].rearrange("p i u r -> p i r u"),
             )
-            d_turned[batch] = grouped[:, :nb * SPAN]
+            d_turned[batch] = grouped
 
         def quantize_d(batch):
             nb = len(batch)
             name = "%d_%d_%d" % batch[0]
             codes = keep.tile([P, nb * P], U32, name="d_codes_" + name, align_bytes=64)
             scales = keep.tile([P, nb * P], U8, name="d_scales_" + name, align_bytes=64)
-            nc.vector.quantize_mx(out=codes[:].bitcast(E4M3X4), scales=scales[:], in_=d_turned[batch])
+            nc.vector.quantize_mx(out=codes[:].bitcast(E4M3X4), scales=scales[:], in_=d_turned[batch][:])
             for i, unit in enumerate(batch):
                 d_codes[unit] = codes[:, i * P:(i + 1) * P]
                 d_scales[unit] = scales[:, i * P:(i + 1) * P]
 
-        y_f32 = [keep.tile([P, PACK, N], F32, name="y_f32_%d" % j) for j in range(CHUNKS)]
-        y_bf16 = [keep.tile([P, N, PACK], BF16, name="y_bf16_%d" % j, align_bytes=64) for j in range(CHUNKS)]
-        y_codes = [keep.tile([P, N], U32, name="y_codes_%d" % j, align_bytes=64) for j in range(CHUNKS)]
+        last = GROUPS - 1
+        y_wide = [keep.tile([P, PACK, RHS], F32, name="y_f32_%d" % g) for g in range(last)]
+        y_half = [keep.tile([P, PACK, N], F32, name="y_f32_last_%d" % h) for h in range(HALVES)]
+        y_bf16 = [keep.tile([P, RHS, PACK], BF16, name="y_bf16_%d" % g, align_bytes=64) for g in range(GROUPS)]
+        y_codes = [keep.tile([P, RHS], U32, name="y_codes_%d" % g, align_bytes=64) for g in range(GROUPS)]
         y_plane = keep.tile([P, GROUPS, RHS], U8, name="y_plane", align_bytes=64)
-        kappa2 = keep.tile([P, P, RHS // P], F32, name="kappa2")
-        kappa2_row = kappa2[:].rearrange("p j m -> p (j m)")
         hop = {}
 
-        def multiply(s):
-            j, t = divmod(s, PACK)
-            g, h = divmod(j, HALVES)
-            bank = hop_ps.tile([P, N], F32, name="hop_bank")
+        def y_f32(g, t0, t1, r0, r1):
+            if g < last:
+                return y_wide[g][:, t0:t1, r0:r1]
+            h = r0 // N
+            return y_half[h][:, t0:t1, r0 - h * N:r1 - h * N]
+
+        def multiply(g, t, h):
+            bank = hop_tile()
             for c in range(PASSES):
                 nc.tensor.matmul_mx(
                     out=bank[:],
@@ -146,136 +214,265 @@ def tile_schur_closing_hop_k2_kernel(tc, d_eo, chi_words, chi_scales, phi, kappa
                     start=(c == 0),
                     stop=(c == PASSES - 1),
                 )
-            hop[s] = bank
+            hop[(g, t, h)] = bank
 
-        def scale(s, n0=0, n1=N):
-            j, t = divmod(s, PACK)
-            h = j % HALVES
+        def scale(g, t, h, n0, n1):
+            r0, r1 = h * N + n0, h * N + n1
             nc.vector.tensor_tensor(
-                out=y_f32[j][:, t, n0:n1], in0=hop[s][:, n0:n1], in1=kappa2_row[:, h * N + n0:h * N + n1], op=ALU.mult
+                out=y_f32(g, t, t + 1, r0, r1)[:, 0, :], in0=hop[(g, t, h)][:, n0:n1], in1=kappa2_row[:, r0:r1], op=ALU.mult
             )
 
-        def subtract(j, t0, t1, n0=0, n1=N):
-            g, h = divmod(j, HALVES)
-            part = y_f32[j][:, t0:t1, n0:n1]
-            src = phi_sb[(g, h, t0 // 2)][:, t0 % 2:t0 % 2 + t1 - t0, n0:n1]
-            nc.vector.tensor_tensor(out=part, in0=src, in1=part, op=ALU.subtract)
+        def subtract(engine, g, t, r0, r1):
+            part = y_f32(g, t, t + 1, r0, r1)[:, 0, :]
+            engine.tensor_tensor(out=part, in0=phi_sb[(g, t)][:, r0:r1], in1=part, op=ALU.subtract)
 
-        def weave_views(j, n0, n1):
-            dst = y_bf16[j][:, n0:n1, :].rearrange("p (c i) t -> p c t i", i=4)
-            src = y_f32[j][:, :, n0:n1].rearrange("p t (c i) -> p c t i", i=4)
-            return dst, src
+        def weave(engine, g, r0, r1):
+            dst = y_bf16[g][:, r0:r1, :].rearrange("p (c i) t -> p c t i", i=4)
+            src = y_f32(g, 0, PACK, r0, r1).rearrange("p t (c i) -> p c t i", i=4)
+            copy_on(engine, dst, src)
 
-        def weave(j, n0, n1):
-            dst, src = weave_views(j, n0, n1)
-            nc.scalar.copy(out=dst, in_=src)
-
-        def quantize_y(j, n0, n1):
-            g, h = divmod(j, HALVES)
+        def quantize_y(g, r0, r1):
             nc.vector.quantize_mx(
-                out=y_codes[j][:, n0:n1].bitcast(E4M3X4),
-                scales=y_plane[:, g, h * N + n0:h * N + n1],
-                in_=y_bf16[j][:, n0:n1, :].rearrange("p n t -> p (n t)"),
+                out=y_codes[g][:, r0:r1].bitcast(E4M3X4),
+                scales=y_plane[:, g, r0:r1],
+                in_=y_bf16[g][:, r0:r1, :].rearrange("p n t -> p (n t)"),
             )
 
-        def store_y(j, t0, t1, n0=0, n1=N):
-            g, h = divmod(j, HALVES)
-            dst = out_0[g * SPAN:(g + 1) * SPAN, h * N + n0:h * N + n1].rearrange("(p t) r -> p t r", t=PACK)
-            nc.sync.dma_start(out=dst[:, t0:t1, :], in_=y_f32[j][:, t0:t1, n0:n1])
+        def store_y(g, t0, t1, r0, r1):
+            dst = out_0[g * SPAN:(g + 1) * SPAN, r0:r1].rearrange("(p t) r -> p t r", t=PACK)
+            nc.sync.dma_start(out=dst[:, t0:t1, :], in_=y_f32(g, t0, t1, r0, r1))
 
-        def store_codes(j):
-            g, h = divmod(j, HALVES)
-            dst = out_1[g].rearrange("p n t -> p (n t)")[:, h * N * PACK:(h + 1) * N * PACK]
-            nc.sync.dma_start(out=dst.bitcast(I32), in_=y_codes[j][:].bitcast(I32))
+        def store_codes(g, r0, r1):
+            dst = out_1[g].rearrange("p n t -> p (n t)")[:, r0 * PACK:r1 * PACK]
+            nc.sync.dma_start(out=dst.bitcast(I32), in_=y_codes[g][:, r0:r1].bitcast(I32))
 
-        def store_plane(g0, g1, queues):
-            for q in range(4):
-                queues[q % len(queues)].dma_start(
-                    out=out_2[g0:g1, 4 * q:4 * q + 4, :].rearrange("g q n -> q g n").bitcast(I32),
-                    in_=y_plane[32 * q:32 * q + 4, g0:g1, :].bitcast(I32),
-                )
+        def store_plane(queue, g0, g1, q):
+            queue.dma_start(
+                out=out_2[g0:g1, 4 * q:4 * q + 4, :].rearrange("g q n -> q g n").bitcast(I32),
+                in_=y_plane[32 * q:32 * q + 4, g0:g1, :].bitcast(I32),
+            )
 
-        kappa2_col = keep.tile([P, RHS // P], F32, name="kappa2_col")
-        nc.vector.tensor_tensor(out=kappa2_col[:], in0=kappa_sb[:], in1=kappa_sb[:], op=ALU.mult)
-        first = [batches(0, t, t + 1) for t in range(PACK)]
-        for b in first[0] + first[1]:
-            turn(b)
-        for m0 in range(0, RHS // P, 4):
-            bank = hop_ps.tile([P, N], F32, name="hop_bank")
-            for m in range(4):
-                nc.tensor.transpose(
-                    bank[:, m * P:(m + 1) * P], kappa2_col[:, m0 + m:m0 + m + 1].to_broadcast([P, P]), ident[:]
-                )
-            nc.scalar.copy(out=kappa2[:, :, m0:m0 + 4], in_=bank[:].rearrange("p (m j) -> p j m", m=4))
-        for b in first[0] + first[1]:
-            quantize_d(b)
-        multiply(0)
-        multiply(1)
-        scale(0)
-        scale(1)
-        subtract(0, 0, 1)
-        for b in first[2]:
-            turn(b)
-            quantize_d(b)
-        subtract(0, 1, 2)
-        for b in first[3]:
-            turn(b)
-            quantize_d(b)
-
-        half = N // 2
-        pending = []
-        for s in range(2, SLOTS - 2):
-            j, t = divmod(s, PACK)
-            g = j // HALVES
-            multiply(s)
-            scale(s)
-            if s % 2 == 0 and s >= 4:
-                jj, tt = divmod(s - 2, PACK)
-                subtract(jj, tt, tt + 2)
-                if tt == 2:
-                    store_y(jj, 0, PACK)
-                    weave(jj, 0, half)
-                for b in pending[:2]:
-                    quantize_d(b)
-                pending = pending[2:]
-            if s % 2 == 1:
-                for b in pending:
-                    quantize_d(b)
-                pending = []
-                if s % 8 in (5, 7) and g + 1 < GROUPS:
-                    pending = batches(g + 1, s % 8 - 5, s % 8 - 3)
-                    for b in pending:
-                        turn(b)
-                if t == 1 and j >= 1:
-                    weave(j - 1, half, N)
-                if t == 3 and j >= 1:
-                    quantize_y(j - 1, 0, half)
-                if t == 1 and j >= 2:
-                    quantize_y(j - 2, half, N)
-                    store_codes(j - 2)
-                    if j - 2 == 2 * HALVES - 1:
-                        store_plane(0, 2, [nc.sync])
-
-        last = CHUNKS - 1
-        multiply(SLOTS - 2)
-        multiply(SLOTS - 1)
-        scale(SLOTS - 2, 0, half)
-        subtract(last, 0, 2)
-        store_y(last, 0, 2)
-        scale(SLOTS - 1, 0, half)
-        scale(SLOTS - 2, half, N)
-        subtract(last, 2, 4, 0, half)
-        weave(last, 0, half)
-        store_y(last, 2, 4, 0, half)
-        scale(SLOTS - 1, half, N)
-        quantize_y(last - 1, 0, half)
-        subtract(last, 2, 4, half, N)
-        store_y(last, 2, 4, half, N)
-        quantize_y(last - 1, half, N)
-        store_codes(last - 1)
-        dst, src = weave_views(last, half, N)
-        nc.vector.tensor_copy(out=dst, in_=src)
-        quantize_y(last, 0, half)
-        quantize_y(last, half, N)
-        store_codes(last)
-        store_plane(2, 3, [nc.scalar, nc.sync])
+        load_d(0, 0, 1)
+        load_d(0, 1, 2)
+        load_chi_scales(0)
+        load_chi_scales(3)
+        load_kappa()
+        load_d(0, 2, 3)
+        load_chi_scales(2)
+        load_chi(0, 0, 1)
+        warm()
+        warm()
+        load_chi_scales(1)
+        split_words(vector, work[0][0])
+        warm()
+        load_chi(0, 1, 3)
+        turn(work[0][0])
+        load_d(0, 3, 4)
+        load_chi(1, 0, 3)
+        load_phi(0, 0)
+        square_kappa()
+        split_words(vector, work[0][2])
+        spread_kappa2(1)
+        gather(work[0][0])
+        turn(work[0][3])
+        load_d(1, 0, 2)
+        spread_kappa2(0)
+        load_phi(0, 1)
+        gather(work[0][3])
+        quantize_d(work[0][0])
+        turn(work[0][2])
+        warm()
+        load_d(1, 2, 4)
+        gather(work[0][2])
+        load_d(2, 0, 2)
+        turn(work[0][1])
+        turn(work[0][5])
+        quantize_d(work[0][2])
+        gather(work[0][1])
+        gather(work[0][5])
+        quantize_d(work[0][1])
+        multiply(0, 0, 0)
+        load_phi(1, 1)
+        copy_kappa2(0)
+        turn(work[0][4])
+        copy_kappa2(1)
+        load_phi(1, 0)
+        scale(0, 0, 0, 0, 512)
+        turn(work[0][6])
+        quantize_d(work[0][3])
+        gather(work[0][4])
+        multiply(0, 1, 0)
+        gather(work[0][6])
+        quantize_d(work[0][4])
+        split_words(scalar, work[0][7])
+        multiply(0, 0, 1)
+        quantize_d(work[0][6])
+        scale(0, 1, 0, 0, 512)
+        multiply(0, 1, 1)
+        quantize_d(work[0][5])
+        scale(0, 0, 1, 0, 512)
+        subtract(gpsimd, 0, 0, 0, 512)
+        multiply(0, 2, 0)
+        scale(0, 1, 1, 0, 512)
+        turn(work[0][7])
+        subtract(vector, 0, 1, 0, 512)
+        turn(work[1][1])
+        split_words(scalar, work[1][0])
+        subtract(vector, 0, 1, 512, 1024)
+        turn(work[1][2])
+        gather(work[0][7])
+        subtract(vector, 0, 0, 512, 1024)
+        gather(work[1][1])
+        turn(work[1][0])
+        multiply(0, 2, 1)
+        scale(0, 2, 0, 0, 512)
+        store_y(0, 0, 2, 0, RHS)
+        gather(work[1][0])
+        quantize_d(work[0][7])
+        quantize_d(work[1][1])
+        gather(work[1][2])
+        multiply(0, 3, 1)
+        quantize_d(work[1][0])
+        scale(0, 2, 1, 0, 512)
+        subtract(gpsimd, 0, 2, 0, 512)
+        split_words(scalar, work[1][5])
+        multiply(0, 3, 0)
+        split_words(scalar, work[1][3])
+        scale(0, 3, 1, 0, 512)
+        split_words(scalar, work[1][4])
+        multiply(1, 0, 0)
+        subtract(vector, 0, 2, 512, 1024)
+        split_words(scalar, work[2][0])
+        scale(0, 3, 0, 0, 512)
+        subtract(gpsimd, 0, 3, 512, 1024)
+        turn(work[1][5])
+        scale(1, 0, 0, 0, 512)
+        turn(work[1][3])
+        gather(work[1][5])
+        turn(work[1][4])
+        multiply(1, 0, 1)
+        subtract(vector, 0, 3, 0, 512)
+        gather(work[1][3])
+        quantize_d(work[1][2])
+        store_y(0, 2, 4, 0, RHS)
+        gather(work[1][4])
+        load_phi(2, 1)
+        quantize_d(work[1][5])
+        load_d(2, 2, 4)
+        multiply(1, 1, 1)
+        load_phi(2, 0)
+        quantize_d(work[1][3])
+        weave(scalar, 0, 0, 256)
+        quantize_d(work[1][4])
+        multiply(1, 2, 0)
+        scale(1, 0, 1, 0, 512)
+        subtract(gpsimd, 1, 0, 0, 512)
+        scale(1, 1, 1, 0, 512)
+        weave(scalar, 0, 256, 512)
+        multiply(1, 1, 0)
+        scale(1, 2, 0, 0, 512)
+        subtract(gpsimd, 1, 0, 512, 1024)
+        turn(work[2][1])
+        scale(1, 1, 0, 0, 512)
+        turn(work[2][0])
+        gather(work[2][1])
+        turn(work[2][2])
+        subtract(vector, 1, 1, 512, 1024)
+        multiply(1, 2, 1)
+        gather(work[2][0])
+        quantize_y(0, 256, 512)
+        subtract(vector, 1, 2, 0, 512)
+        gather(work[2][2])
+        quantize_d(work[2][0])
+        multiply(1, 3, 0)
+        weave(scalar, 0, 768, 1024)
+        quantize_d(work[2][1])
+        quantize_d(work[2][2])
+        multiply(1, 3, 1)
+        scale(1, 2, 1, 0, 512)
+        subtract(gpsimd, 1, 1, 0, 512)
+        weave(scalar, 0, 512, 768)
+        scale(1, 3, 0, 0, 512)
+        multiply(2, 0, 0)
+        scale(1, 3, 1, 0, 512)
+        store_y(1, 0, 2, 0, RHS)
+        turn(work[2][5])
+        subtract(vector, 1, 3, 0, 512)
+        split_words(scalar, work[2][3])
+        turn(work[2][4])
+        subtract(vector, 1, 2, 512, 1024)
+        turn(work[2][3])
+        subtract(vector, 1, 3, 512, 1024)
+        gather(work[2][4])
+        multiply(2, 0, 1)
+        scale(2, 0, 0, 0, 512)
+        store_y(1, 2, 4, 0, RHS)
+        gather(work[2][3])
+        quantize_d(work[2][4])
+        multiply(2, 1, 1)
+        gather(work[2][5])
+        quantize_y(0, 768, 1024)
+        quantize_d(work[2][3])
+        weave(scalar, 1, 768, 1024)
+        multiply(2, 1, 0)
+        quantize_y(0, 512, 768)
+        quantize_y(0, 0, 256)
+        quantize_d(work[2][5])
+        store_codes(0, 0, RHS)
+        multiply(2, 3, 1)
+        scale(2, 1, 1, 0, 512)
+        subtract(gpsimd, 2, 0, 0, 512)
+        weave(scalar, 1, 512, 768)
+        scale(2, 1, 0, 0, 512)
+        multiply(2, 2, 0)
+        scale(2, 0, 1, 0, 512)
+        subtract(gpsimd, 2, 1, 512, 1024)
+        weave(scalar, 1, 0, 256)
+        scale(2, 3, 1, 0, 256)
+        multiply(2, 3, 0)
+        scale(2, 2, 0, 0, 512)
+        subtract(vector, 2, 1, 0, 512)
+        multiply(2, 2, 1)
+        weave(scalar, 1, 256, 512)
+        subtract(vector, 2, 0, 512, 1024)
+        store_y(2, 0, 2, 0, 512)
+        scale(2, 3, 0, 0, 512)
+        subtract(gpsimd, 2, 2, 0, 512)
+        store_y(2, 0, 2, 512, 1024)
+        scale(2, 3, 1, 256, 384)
+        scale(2, 2, 1, 0, 512)
+        subtract(vector, 2, 3, 0, 512)
+        quantize_y(1, 512, 768)
+        weave(scalar, 2, 0, 256)
+        store_y(2, 2, 4, 0, 512)
+        quantize_y(1, 768, 1024)
+        quantize_y(1, 256, 512)
+        quantize_y(1, 0, 256)
+        subtract(vector, 2, 3, 512, 768)
+        store_plane(nc.sync, 0, 2, 1)
+        weave(scalar, 2, 256, 512)
+        store_codes(1, 0, RHS)
+        subtract(vector, 2, 3, 768, 896)
+        store_y(2, 3, 4, 512, 768)
+        scale(2, 3, 1, 384, 512)
+        store_plane(nc.sync, 0, 2, 3)
+        subtract(vector, 2, 2, 512, 1024)
+        subtract(vector, 2, 3, 896, 1024)
+        weave(scalar, 2, 512, 768)
+        weave(vector, 2, 768, 896)
+        store_y(2, 3, 4, 768, 1024)
+        store_plane(nc.sync, 0, 2, 0)
+        store_y(2, 2, 3, 512, 1024)
+        quantize_y(2, 256, 512)
+        store_plane(nc.sync, 0, 2, 2)
+        quantize_y(2, 0, 256)
+        quantize_y(2, 768, 896)
+        store_codes(2, 0, 512)
+        weave(scalar, 2, 896, 1024)
+        quantize_y(2, 512, 768)
+        quantize_y(2, 896, 1024)
+        store_plane(nc.sync, 2, 3, 2)
+        store_codes(2, 512, 1024)
+        store_plane(nc.sync, 2, 3, 0)
+        store_plane(nc.sync, 2, 3, 3)
+        store_plane(nc.sync, 2, 3, 1)

@@ -88,12 +88,12 @@ def tile_schur_closing_hop_k2_kernel(tc, d_eo, chi_words, chi_scales, phi, kappa
             for t in range(t0, t1):
                 d_rows[(g, t)] = raw[:, t - t0, :].bitcast(F32)
 
-        def load_phi(g, pair):
-            raw = keep.tile([P, 2, RHS], BF16, name="phi_%d_%d" % (g, pair))
+        def load_phi(g, t0, t1):
+            raw = keep.tile([P, t1 - t0, RHS], BF16, name="phi_%d_%d" % (g, t0))
             src = phi[g * SPAN:(g + 1) * SPAN, :].rearrange("(p t) r -> p t r", t=PACK)
-            nc.sync.dma_start(out=raw[:], in_=src[:, 2 * pair:2 * pair + 2, :])
-            for i in range(2):
-                phi_sb[(g, 2 * pair + i)] = raw[:, i, :]
+            nc.sync.dma_start(out=raw[:], in_=src[:, t0:t1, :])
+            for t in range(t0, t1):
+                phi_sb[(g, t)] = (raw, t - t0)
 
         def load_chi(h, c0, c1):
             raw = keep.tile([P, c1 - c0, N], U32, name="chi_%d_%d" % (h, c0), align_bytes=64)
@@ -108,11 +108,12 @@ def tile_schur_closing_hop_k2_kernel(tc, d_eo, chi_words, chi_scales, phi, kappa
                 in_=kappa.rearrange("(h p m) -> p h m", p=P, m=PACK),
             )
 
-        def load_chi_scales(q):
-            nc.sync.dma_start(
-                out=chi_plane[32 * q:32 * q + 4, :].rearrange("p (c n) -> p c n", c=PASSES).bitcast(I32),
-                in_=chi_scales[:, 4 * q:4 * q + 4, :].rearrange("c q n -> q c n").bitcast(I32),
-            )
+        def load_chi_scales():
+            for q in range(4):
+                nc.sync.dma_start(
+                    out=chi_plane[32 * q:32 * q + 4, :].rearrange("p (c n) -> p c n", c=PASSES).bitcast(I32),
+                    in_=chi_scales[:, 4 * q:4 * q + 4, :].rearrange("c q n -> q c n").bitcast(I32),
+                )
 
         def square_kappa():
             nc.vector.tensor_tensor(out=kappa2_col[:], in0=kappa_sb[:], in1=kappa_sb[:], op=ALU.mult)
@@ -132,7 +133,8 @@ def tile_schur_closing_hop_k2_kernel(tc, d_eo, chi_words, chi_scales, phi, kappa
 
         units = [[(g, t, c) for t in range(PACK) for c in range(PASSES)] for g in range(GROUPS)]
         work = [[tuple(row[i:i + 2]) for i in range(0, len(row), 2)] for row in units]
-        work[0] = [tuple(units[0][3 * t + a:3 * t + b]) for t in range(PACK) for a, b in ((0, 2), (2, 3))]
+        work[0] = [tuple(units[0][3 * t + a:3 * t + b]) for t in range(2) for a, b in ((0, 2), (2, 3))] + 2 * [()] + work[0][3:]
+        d_stage = {}
         d_split = {}
         d_bank = {}
         d_turned = {}
@@ -171,20 +173,25 @@ def tile_schur_closing_hop_k2_kernel(tc, d_eo, chi_words, chi_scales, phi, kappa
 
         def gather(batch):
             nb = len(batch)
-            grouped = keep.tile([P, nb * SPAN], BF16, name="d_grouped", bufs=7, align_bytes=64)
+            g, t, c = batch[0]
+            if (g, t // 2) not in d_stage:
+                d_stage[(g, t // 2)] = keep.tile([P, 2 * ODD], BF16, name="d_grouped", bufs=3, align_bytes=64)
+            at = (t % 2 * PASSES + c) * SPAN
             nc.scalar.copy(
-                out=grouped[:].bitcast(F32).rearrange("p (i r u) -> p i r u", i=nb, u=2),
+                out=d_stage[(g, t // 2)][:, at:at + nb * SPAN].bitcast(F32).rearrange("p (i r u) -> p i r u", i=nb, u=2),
                 in_=d_bank[batch][:, :nb, :, :].rearrange("p i u r -> p i r u"),
             )
-            d_turned[batch] = grouped
 
-        def quantize_d(batch):
-            nb = len(batch)
-            name = "%d_%d_%d" % batch[0]
-            codes = keep.tile([P, nb * P], U32, name="d_codes_" + name, align_bytes=64)
-            scales = keep.tile([P, nb * P], U8, name="d_scales_" + name, align_bytes=64)
-            nc.vector.quantize_mx(out=codes[:].bitcast(E4M3X4), scales=scales[:], in_=d_turned[batch][:])
-            for i, unit in enumerate(batch):
+        def quantize_d(some):
+            cells = [unit for batch in some for unit in batch]
+            g, t, c = cells[0]
+            name = "%d_%d_%d" % cells[0]
+            codes = keep.tile([P, len(cells) * P], U32, name="d_codes_" + name, align_bytes=64)
+            scales = keep.tile([P, len(cells) * P], U8, name="d_scales_" + name, align_bytes=64)
+            at = (t % 2 * PASSES + c) * SPAN
+            grouped = d_stage[(g, t // 2)][:, at:at + len(cells) * SPAN]
+            nc.vector.quantize_mx(out=codes[:].bitcast(E4M3X4), scales=scales[:], in_=grouped)
+            for i, unit in enumerate(cells):
                 d_codes[unit] = codes[:, i * P:(i + 1) * P]
                 d_scales[unit] = scales[:, i * P:(i + 1) * P]
 
@@ -222,9 +229,15 @@ def tile_schur_closing_hop_k2_kernel(tc, d_eo, chi_words, chi_scales, phi, kappa
                 out=y_f32(g, t, t + 1, r0, r1)[:, 0, :], in0=hop[(g, t, h)][:, n0:n1], in1=kappa2_row[:, r0:r1], op=ALU.mult
             )
 
-        def subtract(engine, g, t, r0, r1):
-            part = y_f32(g, t, t + 1, r0, r1)[:, 0, :]
-            engine.tensor_tensor(out=part, in0=phi_sb[(g, t)][:, r0:r1], in1=part, op=ALU.subtract)
+        def subtract(engine, g, t0, t1, r0, r1):
+            part = y_f32(g, t0, t1, r0, r1)
+            rows, at = phi_sb[(g, t0)]
+            engine.tensor_tensor(out=part, in0=rows[:, at:at + t1 - t0, r0:r1], in1=part, op=ALU.subtract)
+
+        def subtract_rest(engine, g, pair):
+            part = y_f32(g, 2 * pair, 2 * pair + 2, 0, RHS).rearrange("p t r -> p (t r)")[:, N:]
+            rows = phi_sb[(g, 2 * pair)][0][:].rearrange("p t r -> p (t r)")[:, N:]
+            engine.tensor_tensor(out=part, in0=rows, in1=part, op=ALU.subtract)
 
         def weave(engine, g, r0, r1):
             dst = y_bf16[g][:, r0:r1, :].rearrange("p (c i) t -> p c t i", i=4)
@@ -246,233 +259,195 @@ def tile_schur_closing_hop_k2_kernel(tc, d_eo, chi_words, chi_scales, phi, kappa
             dst = out_1[g].rearrange("p n t -> p (n t)")[:, r0 * PACK:r1 * PACK]
             nc.sync.dma_start(out=dst.bitcast(I32), in_=y_codes[g][:, r0:r1].bitcast(I32))
 
-        def store_plane(queue, g0, g1, q):
-            queue.dma_start(
-                out=out_2[g0:g1, 4 * q:4 * q + 4, :].rearrange("g q n -> q g n").bitcast(I32),
-                in_=y_plane[32 * q:32 * q + 4, g0:g1, :].bitcast(I32),
-            )
+        def store_plane(g0, g1, queues):
+            for q in range(4):
+                queues[q % len(queues)].dma_start(
+                    out=out_2[g0:g1, 4 * q:4 * q + 4, :].rearrange("g q n -> q g n").bitcast(I32),
+                    in_=y_plane[32 * q:32 * q + 4, g0:g1, :].bitcast(I32),
+                )
 
+        load_kappa()
         load_d(0, 0, 1)
         load_d(0, 1, 2)
-        load_chi_scales(0)
-        load_chi_scales(3)
-        load_kappa()
-        load_d(0, 2, 3)
-        load_chi_scales(2)
+        load_chi(0, 1, 3)
         load_chi(0, 0, 1)
         warm()
+        load_chi_scales()
         warm()
-        load_chi_scales(1)
+        load_d(0, 2, 3)
         split_words(vector, work[0][0])
+        split_words(scalar, work[0][1])
         warm()
-        load_chi(0, 1, 3)
+        square_kappa()
         turn(work[0][0])
         load_d(0, 3, 4)
-        load_chi(1, 0, 3)
-        load_phi(0, 0)
-        square_kappa()
-        split_words(vector, work[0][2])
-        spread_kappa2(1)
-        gather(work[0][0])
-        turn(work[0][3])
-        load_d(1, 0, 2)
-        spread_kappa2(0)
-        load_phi(0, 1)
-        gather(work[0][3])
-        quantize_d(work[0][0])
+        split_words(vector, work[0][3])
         turn(work[0][2])
-        warm()
-        load_d(1, 2, 4)
-        gather(work[0][2])
-        load_d(2, 0, 2)
+        gather(work[0][0])
+        load_chi(1, 0, 3)
         turn(work[0][1])
-        turn(work[0][5])
-        quantize_d(work[0][2])
+        spread_kappa2(0)
+        gather(work[0][2])
+        quantize_d([work[0][0]])
+        load_phi(0, 0, 2)
+        turn(work[0][3])
+        spread_kappa2(1)
         gather(work[0][1])
-        gather(work[0][5])
-        quantize_d(work[0][1])
-        multiply(0, 0, 0)
-        load_phi(1, 1)
-        copy_kappa2(0)
-        turn(work[0][4])
+        warm()
         copy_kappa2(1)
-        load_phi(1, 0)
-        scale(0, 0, 0, 0, 512)
+        quantize_d([work[0][1]])
+        load_d(1, 0, 2)
+        load_d(1, 2, 4)
+        multiply(0, 0, 0)
+        load_phi(0, 2, 4)
+        load_d(2, 0, 2)
+        gather(work[0][3])
+        copy_kappa2(0)
+        quantize_d([work[0][3]])
         turn(work[0][6])
-        quantize_d(work[0][3])
-        gather(work[0][4])
-        multiply(0, 1, 0)
-        gather(work[0][6])
-        quantize_d(work[0][4])
-        split_words(scalar, work[0][7])
-        multiply(0, 0, 1)
-        quantize_d(work[0][6])
-        scale(0, 1, 0, 0, 512)
-        multiply(0, 1, 1)
-        quantize_d(work[0][5])
-        scale(0, 0, 1, 0, 512)
-        subtract(gpsimd, 0, 0, 0, 512)
-        multiply(0, 2, 0)
-        scale(0, 1, 1, 0, 512)
+        scale(0, 0, 0, 0, 512)
         turn(work[0][7])
-        subtract(vector, 0, 1, 0, 512)
-        turn(work[1][1])
-        split_words(scalar, work[1][0])
-        subtract(vector, 0, 1, 512, 1024)
-        turn(work[1][2])
+        gather(work[0][6])
+        quantize_d([work[0][2]])
+        turn(work[0][8])
         gather(work[0][7])
-        subtract(vector, 0, 0, 512, 1024)
-        gather(work[1][1])
-        turn(work[1][0])
+        multiply(0, 1, 0)
+        gather(work[0][8])
+        quantize_d(work[0][6:8])
+        multiply(0, 1, 1)
+        quantize_d([work[0][8]])
+        scale(0, 1, 0, 0, 512)
+        multiply(0, 0, 1)
+        scale(0, 1, 1, 0, 512)
+        subtract(gpsimd, 0, 0, 1, 0, 512)
+        multiply(0, 3, 0)
+        scale(0, 0, 1, 0, 512)
+        multiply(0, 2, 0)
+        subtract(vector, 0, 1, 2, 0, 512)
+        split_words(scalar, work[1][1])
+        split_words(vector, work[1][2])
         multiply(0, 2, 1)
+        split_words(scalar, work[1][0])
+        subtract(vector, 0, 0, 2, 512, 1024)
+        turn(work[1][1])
+        split_words(scalar, work[1][3])
+        turn(work[1][0])
         scale(0, 2, 0, 0, 512)
         store_y(0, 0, 2, 0, RHS)
-        gather(work[1][0])
-        quantize_d(work[0][7])
-        quantize_d(work[1][1])
-        gather(work[1][2])
+        load_phi(1, 0, 2)
         multiply(0, 3, 1)
-        quantize_d(work[1][0])
+        load_phi(1, 2, 4)
+        gather(work[1][1])
         scale(0, 2, 1, 0, 512)
-        subtract(gpsimd, 0, 2, 0, 512)
-        split_words(scalar, work[1][5])
-        multiply(0, 3, 0)
-        split_words(scalar, work[1][3])
-        scale(0, 3, 1, 0, 512)
-        split_words(scalar, work[1][4])
-        multiply(1, 0, 0)
-        subtract(vector, 0, 2, 512, 1024)
-        split_words(scalar, work[2][0])
+        subtract(gpsimd, 0, 2, 3, 0, 512)
+        gather(work[1][0])
         scale(0, 3, 0, 0, 512)
-        subtract(gpsimd, 0, 3, 512, 1024)
+        turn(work[1][2])
         turn(work[1][5])
-        scale(1, 0, 0, 0, 512)
-        turn(work[1][3])
-        gather(work[1][5])
+        scale(0, 3, 1, 0, 512)
+        gather(work[1][2])
         turn(work[1][4])
-        multiply(1, 0, 1)
-        subtract(vector, 0, 3, 0, 512)
-        gather(work[1][3])
-        quantize_d(work[1][2])
-        store_y(0, 2, 4, 0, RHS)
+        quantize_d(work[1][0:2])
+        gather(work[1][5])
+        turn(work[1][3])
+        quantize_d([work[1][2]])
         gather(work[1][4])
-        load_phi(2, 1)
-        quantize_d(work[1][5])
-        load_d(2, 2, 4)
-        multiply(1, 1, 1)
-        load_phi(2, 0)
-        quantize_d(work[1][3])
-        weave(scalar, 0, 0, 256)
-        quantize_d(work[1][4])
-        multiply(1, 2, 0)
-        scale(1, 0, 1, 0, 512)
-        subtract(gpsimd, 1, 0, 0, 512)
-        scale(1, 1, 1, 0, 512)
-        weave(scalar, 0, 256, 512)
+        multiply(1, 0, 0)
+        subtract_rest(vector, 0, 1)
+        gather(work[1][3])
         multiply(1, 1, 0)
-        scale(1, 2, 0, 0, 512)
-        subtract(gpsimd, 1, 0, 512, 1024)
-        turn(work[2][1])
+        multiply(1, 0, 1)
+        quantize_d([work[1][5]])
+        weave(scalar, 0, 256, 512)
+        store_y(0, 2, 4, 0, RHS)
+        load_d(2, 2, 4)
+        quantize_d(work[1][3:5])
+        multiply(1, 1, 1)
+        scale(1, 0, 0, 0, 512)
+        weave(scalar, 0, 0, 256)
+        multiply(1, 2, 0)
         scale(1, 1, 0, 0, 512)
-        turn(work[2][0])
-        gather(work[2][1])
+        subtract(gpsimd, 1, 0, 1, 0, 512)
+        scale(1, 0, 1, 0, 512)
         turn(work[2][2])
-        subtract(vector, 1, 1, 512, 1024)
-        multiply(1, 2, 1)
-        gather(work[2][0])
-        quantize_y(0, 256, 512)
-        subtract(vector, 1, 2, 0, 512)
+        split_words(scalar, work[2][1])
+        scale(1, 1, 1, 0, 512)
+        turn(work[2][0])
         gather(work[2][2])
-        quantize_d(work[2][0])
+        quantize_y(0, 0, 512)
+        turn(work[2][1])
         multiply(1, 3, 0)
+        gather(work[2][0])
+        subtract_rest(vector, 1, 0)
+        gather(work[2][1])
+        multiply(1, 2, 1)
         weave(scalar, 0, 768, 1024)
-        quantize_d(work[2][1])
-        quantize_d(work[2][2])
+        quantize_d([work[2][2]])
         multiply(1, 3, 1)
-        scale(1, 2, 1, 0, 512)
-        subtract(gpsimd, 1, 1, 0, 512)
-        weave(scalar, 0, 512, 768)
-        scale(1, 3, 0, 0, 512)
-        multiply(2, 0, 0)
-        scale(1, 3, 1, 0, 512)
         store_y(1, 0, 2, 0, RHS)
-        turn(work[2][5])
-        subtract(vector, 1, 3, 0, 512)
-        split_words(scalar, work[2][3])
-        turn(work[2][4])
-        subtract(vector, 1, 2, 512, 1024)
+        load_phi(2, 0, 4)
+        scale(1, 2, 0, 0, 512)
+        weave(scalar, 0, 512, 768)
         turn(work[2][3])
-        subtract(vector, 1, 3, 512, 1024)
-        gather(work[2][4])
-        multiply(2, 0, 1)
-        scale(2, 0, 0, 0, 512)
-        store_y(1, 2, 4, 0, RHS)
+        scale(1, 3, 0, 0, 512)
+        subtract(gpsimd, 1, 2, 3, 0, 512)
+        turn(work[2][4])
+        scale(1, 2, 1, 0, 512)
         gather(work[2][3])
-        quantize_d(work[2][4])
-        multiply(2, 1, 1)
+        turn(work[2][5])
+        scale(1, 3, 1, 0, 512)
+        gather(work[2][4])
+        quantize_d(work[2][0:2])
         gather(work[2][5])
-        quantize_y(0, 768, 1024)
-        quantize_d(work[2][3])
-        weave(scalar, 1, 768, 1024)
+        subtract_rest(vector, 1, 1)
+        multiply(2, 0, 0)
         multiply(2, 1, 0)
-        quantize_y(0, 512, 768)
-        quantize_y(0, 0, 256)
-        quantize_d(work[2][5])
-        store_codes(0, 0, RHS)
-        multiply(2, 3, 1)
-        scale(2, 1, 1, 0, 512)
-        subtract(gpsimd, 2, 0, 0, 512)
-        weave(scalar, 1, 512, 768)
-        scale(2, 1, 0, 0, 512)
-        multiply(2, 2, 0)
-        scale(2, 0, 1, 0, 512)
-        subtract(gpsimd, 2, 1, 512, 1024)
+        quantize_d(work[2][3:5])
         weave(scalar, 1, 0, 256)
-        scale(2, 3, 1, 0, 256)
+        store_y(1, 2, 4, 0, RHS)
+        quantize_d([work[2][5]])
         multiply(2, 3, 0)
-        scale(2, 2, 0, 0, 512)
-        subtract(vector, 2, 1, 0, 512)
-        multiply(2, 2, 1)
+        quantize_y(0, 512, 1024)
+        weave(scalar, 1, 768, 1024)
+        scale(2, 0, 0, 0, 512)
+        multiply(2, 2, 0)
+        store_codes(0, 0, RHS)
+        scale(2, 1, 0, 0, 512)
+        subtract(gpsimd, 2, 0, 1, 0, 512)
+        multiply(2, 3, 1)
         weave(scalar, 1, 256, 512)
-        subtract(vector, 2, 0, 512, 1024)
-        store_y(2, 0, 2, 0, 512)
         scale(2, 3, 0, 0, 512)
-        subtract(gpsimd, 2, 2, 0, 512)
-        store_y(2, 0, 2, 512, 1024)
-        scale(2, 3, 1, 256, 384)
-        scale(2, 2, 1, 0, 512)
-        subtract(vector, 2, 3, 0, 512)
-        quantize_y(1, 512, 768)
+        multiply(2, 1, 1)
+        scale(2, 2, 0, 0, 512)
+        weave(scalar, 1, 512, 768)
+        scale(2, 3, 1, 0, 256)
+        multiply(2, 2, 1)
+        subtract(vector, 2, 1, 4, 0, 512)
+        multiply(2, 0, 1)
+        quantize_y(1, 0, 512)
         weave(scalar, 2, 0, 256)
-        store_y(2, 2, 4, 0, 512)
-        quantize_y(1, 768, 1024)
-        quantize_y(1, 256, 512)
-        quantize_y(1, 0, 256)
-        subtract(vector, 2, 3, 512, 768)
-        store_plane(nc.sync, 0, 2, 1)
-        weave(scalar, 2, 256, 512)
+        store_y(2, 0, 4, 0, 512)
+        quantize_y(1, 512, 1024)
+        scale(2, 0, 1, 0, 512)
         store_codes(1, 0, RHS)
-        subtract(vector, 2, 3, 768, 896)
-        store_y(2, 3, 4, 512, 768)
-        scale(2, 3, 1, 384, 512)
-        store_plane(nc.sync, 0, 2, 3)
-        subtract(vector, 2, 2, 512, 1024)
-        subtract(vector, 2, 3, 896, 1024)
+        weave(scalar, 2, 256, 512)
+        store_plane(0, 2, [nc.sync])
+        scale(2, 1, 1, 0, 512)
+        subtract(gpsimd, 2, 0, 1, 512, 1024)
+        scale(2, 3, 1, 256, 512)
+        scale(2, 2, 1, 0, 512)
+        subtract(vector, 2, 3, 4, 512, 768)
+        store_y(2, 0, 1, 512, 1024)
+        subtract(vector, 2, 1, 3, 512, 1024)
+        subtract(vector, 2, 3, 4, 768, 1024)
         weave(scalar, 2, 512, 768)
+        store_y(2, 1, 3, 512, 1024)
+        quantize_y(2, 0, 512)
         weave(vector, 2, 768, 896)
-        store_y(2, 3, 4, 768, 1024)
-        store_plane(nc.sync, 0, 2, 0)
-        store_y(2, 2, 3, 512, 1024)
-        quantize_y(2, 256, 512)
-        store_plane(nc.sync, 0, 2, 2)
-        quantize_y(2, 0, 256)
-        quantize_y(2, 768, 896)
         store_codes(2, 0, 512)
-        weave(scalar, 2, 896, 1024)
+        store_y(2, 3, 4, 512, 1024)
+        weave(vector, 2, 896, 1024)
         quantize_y(2, 512, 768)
-        quantize_y(2, 896, 1024)
-        store_plane(nc.sync, 2, 3, 2)
+        quantize_y(2, 768, 1024)
         store_codes(2, 512, 1024)
-        store_plane(nc.sync, 2, 3, 0)
-        store_plane(nc.sync, 2, 3, 3)
-        store_plane(nc.sync, 2, 3, 1)
+        store_plane(2, 3, [nc.sync, nc.scalar])

@@ -49,17 +49,19 @@ def tile_schur_closing_hop_k2_kernel(tc, d_eo, chi_words, chi_scales, phi, kappa
             hop_count.append(0)
             return psum.tile([P, N], F32, name="hop_bank_%d" % ((len(hop_count) - 1) % HOP_BANKS))
 
-        ident = keep.tile([P, P], F32, name="ident")
-        make_identity(nc, ident[:])
-
-        zeros = keep.tile([P, PACK * N], BF16, name="zeros", align_bytes=64)
+        zeros = keep.tile([P, SPAN], BF16, name="zeros", align_bytes=64)
         nc.vector.memset(zeros[:].bitcast(I32), 0)
-        chi_plane = keep.tile([P, PASSES * RHS], U8, name="chi_plane", align_bytes=64)
-        nc.vector.memset(chi_plane[:].bitcast(I32), 0)
         warm_codes = keep.tile([P, N + P], U32, name="warm_codes", align_bytes=64)
         warm_scales = keep.tile([P, N + P], U8, name="warm_scales", align_bytes=64)
-        nc.vector.quantize_mx(out=warm_codes[:, :N].bitcast(E5M2X4), scales=warm_scales[:, :N], in_=zeros[:])
-        nc.vector.quantize_mx(out=warm_codes[:, N:].bitcast(E4M3X4), scales=warm_scales[:, N:], in_=zeros[:, :SPAN])
+        for n0 in range(0, N, P):
+            cols = slice(n0, n0 + P)
+            nc.vector.quantize_mx(out=warm_codes[:, cols].bitcast(E5M2X4), scales=warm_scales[:, cols], in_=zeros[:])
+        nc.vector.quantize_mx(out=warm_codes[:, N:].bitcast(E4M3X4), scales=warm_scales[:, N:], in_=zeros[:])
+        chi_plane = keep.tile([P, PASSES * RHS], U8, name="chi_plane", align_bytes=64)
+        nc.vector.memset(chi_plane[:].bitcast(I32), 0)
+        ident = keep.tile([P, P], F32, name="ident")
+        nc.vector.memset(ident[:], 0.0)
+        make_identity(nc, ident[:], nomemset=True)
         warm_bank = hop_tile()
 
         def warm():
@@ -174,11 +176,11 @@ def tile_schur_closing_hop_k2_kernel(tc, d_eo, chi_words, chi_scales, phi, kappa
         def gather(batch):
             nb = len(batch)
             g, t, c = batch[0]
-            if (g, t // 2) not in d_stage:
-                d_stage[(g, t // 2)] = keep.tile([P, 2 * ODD], BF16, name="d_grouped", bufs=3, align_bytes=64)
-            at = (t % 2 * PASSES + c) * SPAN
+            if g not in d_stage:
+                d_stage[g] = keep.tile([P, PACK * ODD], BF16, name="d_grouped", bufs=2, align_bytes=64)
+            at = (t * PASSES + c) * SPAN
             nc.scalar.copy(
-                out=d_stage[(g, t // 2)][:, at:at + nb * SPAN].bitcast(F32).rearrange("p (i r u) -> p i r u", i=nb, u=2),
+                out=d_stage[g][:, at:at + nb * SPAN].bitcast(F32).rearrange("p (i r u) -> p i r u", i=nb, u=2),
                 in_=d_bank[batch][:, :nb, :, :].rearrange("p i u r -> p i r u"),
             )
 
@@ -188,8 +190,8 @@ def tile_schur_closing_hop_k2_kernel(tc, d_eo, chi_words, chi_scales, phi, kappa
             name = "%d_%d_%d" % cells[0]
             codes = keep.tile([P, len(cells) * P], U32, name="d_codes_" + name, align_bytes=64)
             scales = keep.tile([P, len(cells) * P], U8, name="d_scales_" + name, align_bytes=64)
-            at = (t % 2 * PASSES + c) * SPAN
-            grouped = d_stage[(g, t // 2)][:, at:at + len(cells) * SPAN]
+            at = (t * PASSES + c) * SPAN
+            grouped = d_stage[g][:, at:at + len(cells) * SPAN]
             nc.vector.quantize_mx(out=codes[:].bitcast(E4M3X4), scales=scales[:], in_=grouped)
             for i, unit in enumerate(cells):
                 d_codes[unit] = codes[:, i * P:(i + 1) * P]
@@ -266,188 +268,190 @@ def tile_schur_closing_hop_k2_kernel(tc, d_eo, chi_words, chi_scales, phi, kappa
                     in_=y_plane[32 * q:32 * q + 4, g0:g1, :].bitcast(I32),
                 )
 
-        load_kappa()
         load_d(0, 0, 1)
         load_d(0, 1, 2)
+        load_kappa()
         load_chi(0, 1, 3)
-        load_chi(0, 0, 1)
         warm()
         load_chi_scales()
         warm()
-        load_d(0, 2, 3)
-        split_words(vector, work[0][0])
-        split_words(scalar, work[0][1])
         warm()
-        square_kappa()
-        turn(work[0][0])
+        load_chi(0, 0, 1)
+        split_words(vector, work[0][0])
+        warm()
+        load_d(0, 2, 3)
+        split_words(scalar, work[0][2])
         load_d(0, 3, 4)
+        turn(work[0][0])
+        square_kappa()
         split_words(vector, work[0][3])
-        turn(work[0][2])
-        gather(work[0][0])
-        load_chi(1, 0, 3)
-        turn(work[0][1])
         spread_kappa2(0)
+        split_words(scalar, work[0][1])
+        turn(work[0][3])
+        gather(work[0][0])
+        turn(work[0][2])
+        load_chi(1, 0, 3)
+        spread_kappa2(1)
         gather(work[0][2])
         quantize_d([work[0][0]])
+        turn(work[0][1])
+        warm()
         load_phi(0, 0, 2)
-        turn(work[0][3])
-        spread_kappa2(1)
+        load_d(1, 0, 2)
         gather(work[0][1])
         warm()
-        copy_kappa2(1)
-        quantize_d([work[0][1]])
-        load_d(1, 0, 2)
-        load_d(1, 2, 4)
-        multiply(0, 0, 0)
         load_phi(0, 2, 4)
-        load_d(2, 0, 2)
-        gather(work[0][3])
+        load_d(1, 2, 4)
+        warm()
         copy_kappa2(0)
+        quantize_d([work[0][1]])
+        load_d(2, 2, 4)
+        multiply(0, 0, 0)
+        gather(work[0][3])
+        copy_kappa2(1)
+        load_phi(1, 0, 2)
         quantize_d([work[0][3]])
         turn(work[0][6])
-        scale(0, 0, 0, 0, 512)
-        turn(work[0][7])
-        gather(work[0][6])
         quantize_d([work[0][2]])
+        turn(work[0][7])
+        load_phi(1, 2, 4)
+        split_words(vector, work[0][8])
+        gather(work[0][6])
+        scale(0, 0, 0, 0, 512)
         turn(work[0][8])
         gather(work[0][7])
         multiply(0, 1, 0)
         gather(work[0][8])
         quantize_d(work[0][6:8])
-        multiply(0, 1, 1)
+        load_d(2, 0, 2)
+        multiply(0, 0, 1)
         quantize_d([work[0][8]])
         scale(0, 1, 0, 0, 512)
-        multiply(0, 0, 1)
-        scale(0, 1, 1, 0, 512)
+        multiply(0, 1, 1)
+        load_phi(2, 0, 4)
         subtract(gpsimd, 0, 0, 1, 0, 512)
-        multiply(0, 3, 0)
         scale(0, 0, 1, 0, 512)
         multiply(0, 2, 0)
-        subtract(vector, 0, 1, 2, 0, 512)
+        scale(0, 1, 1, 0, 512)
+        multiply(0, 3, 0)
         split_words(scalar, work[1][1])
-        split_words(vector, work[1][2])
-        multiply(0, 2, 1)
+        subtract(vector, 0, 1, 2, 0, 512)
         split_words(scalar, work[1][0])
-        subtract(vector, 0, 0, 2, 512, 1024)
-        turn(work[1][1])
-        split_words(scalar, work[1][3])
-        turn(work[1][0])
         scale(0, 2, 0, 0, 512)
-        store_y(0, 0, 2, 0, RHS)
-        load_phi(1, 0, 2)
+        multiply(0, 2, 1)
+        split_words(scalar, work[1][2])
+        subtract(vector, 0, 0, 2, 512, 1024)
+        turn(work[1][0])
+        turn(work[1][1])
+        subtract(gpsimd, 0, 2, 3, 0, 512)
+        scale(0, 3, 0, 0, 512)
+        gather(work[1][0])
         multiply(0, 3, 1)
-        load_phi(1, 2, 4)
         gather(work[1][1])
         scale(0, 2, 1, 0, 512)
-        subtract(gpsimd, 0, 2, 3, 0, 512)
-        gather(work[1][0])
-        scale(0, 3, 0, 0, 512)
         turn(work[1][2])
-        turn(work[1][5])
+        split_words(scalar, work[1][5])
         scale(0, 3, 1, 0, 512)
-        gather(work[1][2])
         turn(work[1][4])
+        gather(work[1][2])
         quantize_d(work[1][0:2])
-        gather(work[1][5])
         turn(work[1][3])
-        quantize_d([work[1][2]])
         gather(work[1][4])
-        multiply(1, 0, 0)
+        turn(work[1][5])
         subtract_rest(vector, 0, 1)
+        multiply(1, 0, 0)
         gather(work[1][3])
-        multiply(1, 1, 0)
+        split_words(scalar, work[2][3])
         multiply(1, 0, 1)
-        quantize_d([work[1][5]])
-        weave(scalar, 0, 256, 512)
+        gather(work[1][5])
+        quantize_d(work[1][2:4])
         store_y(0, 2, 4, 0, RHS)
-        load_d(2, 2, 4)
-        quantize_d(work[1][3:5])
-        multiply(1, 1, 1)
-        scale(1, 0, 0, 0, 512)
+        store_y(0, 0, 2, 0, RHS)
+        multiply(1, 1, 0)
         weave(scalar, 0, 0, 256)
-        multiply(1, 2, 0)
-        scale(1, 1, 0, 0, 512)
-        subtract(gpsimd, 1, 0, 1, 0, 512)
+        scale(1, 0, 0, 0, 512)
         scale(1, 0, 1, 0, 512)
-        turn(work[2][2])
-        split_words(scalar, work[2][1])
+        multiply(1, 1, 1)
+        subtract(gpsimd, 1, 0, 1, 0, 512)
+        weave(scalar, 0, 512, 768)
+        scale(1, 1, 0, 0, 512)
+        turn(work[2][1])
         scale(1, 1, 1, 0, 512)
         turn(work[2][0])
-        gather(work[2][2])
-        quantize_y(0, 0, 512)
-        turn(work[2][1])
-        multiply(1, 3, 0)
-        gather(work[2][0])
-        subtract_rest(vector, 1, 0)
-        gather(work[2][1])
-        multiply(1, 2, 1)
         weave(scalar, 0, 768, 1024)
-        quantize_d([work[2][2]])
-        multiply(1, 3, 1)
-        store_y(1, 0, 2, 0, RHS)
-        load_phi(2, 0, 4)
+        quantize_d(work[1][4:6])
+        multiply(1, 2, 0)
+        subtract_rest(vector, 1, 0)
+        split_words(scalar, work[2][4])
+        multiply(1, 2, 1)
+        gather(work[2][1])
+        multiply(1, 3, 0)
         scale(1, 2, 0, 0, 512)
-        weave(scalar, 0, 512, 768)
-        turn(work[2][3])
-        scale(1, 3, 0, 0, 512)
-        subtract(gpsimd, 1, 2, 3, 0, 512)
-        turn(work[2][4])
+        weave(scalar, 0, 256, 512)
+        store_y(1, 0, 2, 0, RHS)
         scale(1, 2, 1, 0, 512)
-        gather(work[2][3])
-        turn(work[2][5])
+        multiply(1, 3, 1)
+        subtract(gpsimd, 1, 2, 3, 0, 512)
+        scale(1, 3, 0, 0, 512)
+        gather(work[2][0])
+        turn(work[2][3])
         scale(1, 3, 1, 0, 512)
-        gather(work[2][4])
+        turn(work[2][2])
+        gather(work[2][3])
+        turn(work[2][4])
         quantize_d(work[2][0:2])
-        gather(work[2][5])
+        gather(work[2][2])
+        turn(work[2][5])
         subtract_rest(vector, 1, 1)
         multiply(2, 0, 0)
+        gather(work[2][5])
+        gather(work[2][4])
+        quantize_d(work[2][2:4])
         multiply(2, 1, 0)
-        quantize_d(work[2][3:5])
-        weave(scalar, 1, 0, 256)
         store_y(1, 2, 4, 0, RHS)
-        quantize_d([work[2][5]])
-        multiply(2, 3, 0)
-        quantize_y(0, 512, 1024)
-        weave(scalar, 1, 768, 1024)
-        scale(2, 0, 0, 0, 512)
-        multiply(2, 2, 0)
-        store_codes(0, 0, RHS)
-        scale(2, 1, 0, 0, 512)
-        subtract(gpsimd, 2, 0, 1, 0, 512)
-        multiply(2, 3, 1)
         weave(scalar, 1, 256, 512)
+        quantize_d(work[2][4:6])
+        quantize_y(0, 0, 1024)
+        multiply(2, 3, 0)
+        weave(scalar, 1, 512, 768)
+        multiply(2, 3, 1)
+        scale(2, 0, 0, 0, 512)
+        store_codes(0, 0, RHS)
+        weave(scalar, 1, 0, 256)
+        scale(2, 1, 0, 0, 512)
+        multiply(2, 2, 0)
+        subtract(gpsimd, 2, 0, 1, 0, 512)
         scale(2, 3, 0, 0, 512)
         multiply(2, 1, 1)
+        weave(scalar, 1, 768, 1024)
         scale(2, 2, 0, 0, 512)
-        weave(scalar, 1, 512, 768)
-        scale(2, 3, 1, 0, 256)
         multiply(2, 2, 1)
+        scale(2, 3, 1, 0, 256)
         subtract(vector, 2, 1, 4, 0, 512)
         multiply(2, 0, 1)
-        quantize_y(1, 0, 512)
+        scale(2, 0, 1, 0, 512)
         weave(scalar, 2, 0, 256)
         store_y(2, 0, 4, 0, 512)
-        quantize_y(1, 512, 1024)
-        scale(2, 0, 1, 0, 512)
-        store_codes(1, 0, RHS)
+        quantize_y(1, 0, 1024)
         weave(scalar, 2, 256, 512)
-        store_plane(0, 2, [nc.sync])
-        scale(2, 1, 1, 0, 512)
         subtract(gpsimd, 2, 0, 1, 512, 1024)
-        scale(2, 3, 1, 256, 512)
         scale(2, 2, 1, 0, 512)
-        subtract(vector, 2, 3, 4, 512, 768)
+        store_codes(1, 0, RHS)
+        scale(2, 3, 1, 256, 512)
+        scale(2, 1, 1, 0, 512)
         store_y(2, 0, 1, 512, 1024)
+        store_plane(0, 2, [nc.sync])
+        subtract(vector, 2, 3, 4, 512, 768)
         subtract(vector, 2, 1, 3, 512, 1024)
         subtract(vector, 2, 3, 4, 768, 1024)
         weave(scalar, 2, 512, 768)
         store_y(2, 1, 3, 512, 1024)
-        quantize_y(2, 0, 512)
-        weave(vector, 2, 768, 896)
-        store_codes(2, 0, 512)
         store_y(2, 3, 4, 512, 1024)
         weave(vector, 2, 896, 1024)
+        quantize_y(2, 0, 512)
+        weave(scalar, 2, 768, 896)
         quantize_y(2, 512, 768)
+        store_codes(2, 0, 512)
         quantize_y(2, 768, 1024)
         store_codes(2, 512, 1024)
         store_plane(2, 3, [nc.sync, nc.scalar])

@@ -21,13 +21,14 @@ SPAN = P * PACK
 GROUPS = EVEN // SPAN
 PASSES = ODD // SPAN
 N = 512
-HALVES = RHS // N
-CHUNKS = GROUPS * HALVES
-SLOTS = CHUNKS * PACK
-
+QUARTER = N // 2
+PAIRS = SPAN // 2
+QUADRANTS = 4
 
 TURN_BANKS = 3
 HOP_BANKS = 5
+SPLIT_TILES = 5
+STAGE_TILES = 2
 
 
 def tile_schur_closing_hop_k2_kernel(tc, d_eo, chi_words, chi_scales, phi, kappa, out_0, out_1, out_2):
@@ -38,16 +39,24 @@ def tile_schur_closing_hop_k2_kernel(tc, d_eo, chi_words, chi_scales, phi, kappa
         psum = ctx.enter_context(tc.psum_pool(name="psum", bufs=1))
         ctx.enter_context(tc.manual_schedule())
 
-        turn_count = []
-        hop_count = []
+        turn_tiles = []
+        hop_tiles = []
 
         def turn_tile():
-            turn_count.append(0)
-            return psum.tile([P, 2, 2, P], F32, name="turn_bank_%d" % ((len(turn_count) - 1) % TURN_BANKS))
+            bank = psum.tile([P, 2, 2, P], F32, name="turn_bank_%d" % (len(turn_tiles) % TURN_BANKS))
+            turn_tiles.append(bank)
+            return bank
 
         def hop_tile():
-            hop_count.append(0)
-            return psum.tile([P, N], F32, name="hop_bank_%d" % ((len(hop_count) - 1) % HOP_BANKS))
+            bank = psum.tile([P, N], F32, name="hop_bank_%d" % (len(hop_tiles) % HOP_BANKS))
+            hop_tiles.append(bank)
+            return bank
+
+        def copy_on(engine, out, in_):
+            if engine is scalar:
+                nc.scalar.copy(out=out, in_=in_)
+            else:
+                nc.vector.tensor_copy(out=out, in_=in_)
 
         zeros = keep.tile([P, SPAN], BF16, name="zeros", align_bytes=64)
         nc.vector.memset(zeros[:].bitcast(I32), 0)
@@ -57,68 +66,81 @@ def tile_schur_closing_hop_k2_kernel(tc, d_eo, chi_words, chi_scales, phi, kappa
             cols = slice(n0, n0 + P)
             nc.vector.quantize_mx(out=warm_codes[:, cols].bitcast(E5M2X4), scales=warm_scales[:, cols], in_=zeros[:])
         nc.vector.quantize_mx(out=warm_codes[:, N:].bitcast(E4M3X4), scales=warm_scales[:, N:], in_=zeros[:])
+        warm_bank = hop_tile()
+
+        def warm(count):
+            for repeat in range(count):
+                nc.tensor.matmul_mx(
+                    out=warm_bank[:],
+                    lhsT=warm_codes[:, N:].bitcast(E4M3X4),
+                    lhsT_scale=warm_scales[:, N:],
+                    rhs=warm_codes[:, :N].bitcast(E5M2X4),
+                    rhs_scale=warm_scales[:, :N],
+                    start=True,
+                    stop=True,
+                )
+
         chi_plane = keep.tile([P, PASSES * RHS], U8, name="chi_plane", align_bytes=64)
         nc.vector.memset(chi_plane[:].bitcast(I32), 0)
         ident = keep.tile([P, P], F32, name="ident")
         nc.vector.memset(ident[:], 0.0)
         make_identity(nc, ident[:], nomemset=True)
-        warm_bank = hop_tile()
 
-        def warm():
-            nc.tensor.matmul_mx(
-                out=warm_bank[:],
-                lhsT=warm_codes[:, N:].bitcast(E4M3X4),
-                lhsT_scale=warm_scales[:, N:],
-                rhs=warm_codes[:, :N].bitcast(E5M2X4),
-                rhs_scale=warm_scales[:, :N],
-                start=True,
-                stop=True,
-            )
-
-        d_rows = {}
-        phi_sb = {}
-        chi_sb = {}
+        d_words = {}
+        phi_rows = {}
+        chi_codes = {}
         kappa_sb = keep.tile([P, RHS // P], BF16, name="kappa_sb")
-        kappa2_col = keep.tile([P, RHS // P], F32, name="kappa2_col")
-        kappa2_row = keep.tile([P, RHS], F32, name="kappa2_row")
-        kappa2_bank = {}
 
         def load_d(g, t0, t1):
             raw = keep.tile([P, t1 - t0, ODD], BF16, name="d_raw_%d_%d" % (g, t0))
             src = d_eo[g * SPAN:(g + 1) * SPAN, :].rearrange("(p t) k -> p t k", t=PACK)
             nc.sync.dma_start(out=raw[:], in_=src[:, t0:t1, :])
             for t in range(t0, t1):
-                d_rows[(g, t)] = raw[:, t - t0, :].bitcast(F32)
+                d_words[(g, t)] = raw[:, t - t0, :].bitcast(F32)
 
         def load_phi(g, t0, t1):
             raw = keep.tile([P, t1 - t0, RHS], BF16, name="phi_%d_%d" % (g, t0))
             src = phi[g * SPAN:(g + 1) * SPAN, :].rearrange("(p t) r -> p t r", t=PACK)
             nc.sync.dma_start(out=raw[:], in_=src[:, t0:t1, :])
             for t in range(t0, t1):
-                phi_sb[(g, t)] = (raw, t - t0)
+                phi_rows[(g, t)] = (raw, t - t0)
 
         def load_chi(h, c0, c1):
             raw = keep.tile([P, c1 - c0, N], U32, name="chi_%d_%d" % (h, c0), align_bytes=64)
-            src = chi_words.rearrange("c p n t -> p c (n t)")[:, c0:c1, h * N * PACK:(h + 1) * N * PACK]
+            src = chi_words.rearrange("c p n i -> p c (n i)")[:, c0:c1, h * N * PACK:(h + 1) * N * PACK]
             nc.sync.dma_start(out=raw[:].bitcast(I32), in_=src.bitcast(I32))
             for c in range(c0, c1):
-                chi_sb[(h, c)] = raw[:, c - c0, :]
+                chi_codes[(h, c)] = raw[:, c - c0, :]
 
-        def load_kappa():
+        load_d(0, 0, 1)
+        nc.sync.dma_start(
+            out=kappa_sb[:].rearrange("p (h m) -> p h m", m=PACK),
+            in_=kappa.rearrange("(h p m) -> p h m", p=P, m=PACK),
+        )
+        load_d(0, 1, 2)
+        load_chi(0, 0, 1)
+        for q in range(QUADRANTS):
             nc.sync.dma_start(
-                out=kappa_sb[:].rearrange("p (h m) -> p h m", m=PACK),
-                in_=kappa.rearrange("(h p m) -> p h m", p=P, m=PACK),
+                out=chi_plane[32 * q:32 * q + 4, :].rearrange("p (c n) -> p c n", c=PASSES).bitcast(I32),
+                in_=chi_scales[:, 4 * q:4 * q + 4, :].rearrange("c q n -> q c n").bitcast(I32),
             )
+        load_chi(0, 1, PASSES)
+        load_d(0, 2, 3)
+        load_d(0, 3, 4)
+        load_chi(1, 0, PASSES)
+        load_phi(0, 0, 2)
+        load_d(1, 0, 2)
+        load_phi(0, 2, 4)
+        load_d(1, 2, 4)
+        load_phi(1, 0, 2)
+        load_phi(1, 2, 4)
+        load_d(2, 0, 2)
+        load_d(2, 2, 4)
+        load_phi(2, 0, 4)
 
-        def load_chi_scales():
-            for q in range(4):
-                nc.sync.dma_start(
-                    out=chi_plane[32 * q:32 * q + 4, :].rearrange("p (c n) -> p c n", c=PASSES).bitcast(I32),
-                    in_=chi_scales[:, 4 * q:4 * q + 4, :].rearrange("c q n -> q c n").bitcast(I32),
-                )
-
-        def square_kappa():
-            nc.vector.tensor_tensor(out=kappa2_col[:], in0=kappa_sb[:], in1=kappa_sb[:], op=ALU.mult)
+        kappa2_col = keep.tile([P, RHS // P], F32, name="kappa2_col")
+        kappa2_row = keep.tile([P, RHS], F32, name="kappa2_row")
+        kappa2_bank = {}
 
         def spread_kappa2(h):
             bank = hop_tile()
@@ -133,33 +155,28 @@ def tile_schur_closing_hop_k2_kernel(tc, d_eo, chi_words, chi_scales, phi, kappa
                 in_=kappa2_bank[h][:].rearrange("p (m j) -> p j m", m=PACK),
             )
 
-        units = [[(g, t, c) for t in range(PACK) for c in range(PASSES)] for g in range(GROUPS)]
-        work = [[tuple(row[i:i + 2]) for i in range(0, len(row), 2)] for row in units]
-        work[0] = [tuple(units[0][3 * t + a:3 * t + b]) for t in range(2) for a, b in ((0, 2), (2, 3))] + 2 * [()] + work[0][3:]
-        d_stage = {}
+        cells = [[(g, t, c) for t in range(PACK) for c in range(PASSES)] for g in range(GROUPS)]
+        batches = [[tuple(row[i:i + 2]) for i in range(0, len(row), 2)] for row in cells]
+        slot0 = [tuple(cells[0][0:2]), tuple(cells[0][2:3])]
+        slot1 = [tuple(cells[0][3:5]), tuple(cells[0][5:6])]
+        slots23 = batches[0][3:]
         d_split = {}
         d_bank = {}
-        d_turned = {}
+        d_stage = {}
         d_codes = {}
         d_scales = {}
 
-        def copy_on(engine, out, in_):
-            if engine is scalar:
-                nc.scalar.copy(out=out, in_=in_)
-            else:
-                nc.vector.tensor_copy(out=out, in_=in_)
-
         def split_words(engine, batch):
             g, t, c = batch[0]
-            nb = len(batch)
-            split = keep.tile([P, nb, 2, P], F32, name="d_split", bufs=5)
+            count = len(batch)
+            split = keep.tile([P, count, 2, P], F32, name="d_split", bufs=SPLIT_TILES)
             if batch[-1][1] == t:
-                src = d_rows[(g, t)][:, 256 * c:256 * (c + nb)]
-                copy_on(engine, split[:], src.rearrange("p (i r u) -> p i u r", i=nb, u=2))
+                src = d_words[(g, t)][:, PAIRS * c:PAIRS * (c + count)]
+                copy_on(engine, split[:], src.rearrange("p (i w u) -> p i u w", i=count, u=2))
             else:
                 for i, (g, t, c) in enumerate(batch):
-                    src = d_rows[(g, t)][:, 256 * c:256 * (c + 1)]
-                    copy_on(engine, split[:, i, :, :], src.rearrange("p (r u) -> p u r", u=2))
+                    src = d_words[(g, t)][:, PAIRS * c:PAIRS * (c + 1)]
+                    copy_on(engine, split[:, i, :, :], src.rearrange("p (w u) -> p u w", u=2))
             d_split[batch] = split
 
         def turn(batch):
@@ -169,37 +186,42 @@ def tile_schur_closing_hop_k2_kernel(tc, d_eo, chi_words, chi_scales, phi, kappa
                     if batch in d_split:
                         words = d_split[batch][:, i, u, :]
                     else:
-                        words = d_rows[(g, t)][:, 256 * c + u:256 * (c + 1):2]
+                        words = d_words[(g, t)][:, PAIRS * c + u:PAIRS * (c + 1):2]
                     nc.tensor.transpose(bank[:, i, u, :], words, ident[:])
             d_bank[batch] = bank
 
         def gather(batch):
-            nb = len(batch)
+            count = len(batch)
             g, t, c = batch[0]
             if g not in d_stage:
-                d_stage[g] = keep.tile([P, PACK * ODD], BF16, name="d_grouped", bufs=2, align_bytes=64)
+                d_stage[g] = keep.tile([P, PACK * ODD], BF16, name="d_grouped", bufs=STAGE_TILES, align_bytes=64)
             at = (t * PASSES + c) * SPAN
             nc.scalar.copy(
-                out=d_stage[g][:, at:at + nb * SPAN].bitcast(F32).rearrange("p (i r u) -> p i r u", i=nb, u=2),
-                in_=d_bank[batch][:, :nb, :, :].rearrange("p i u r -> p i r u"),
+                out=d_stage[g][:, at:at + count * SPAN].bitcast(F32).rearrange("p (i r u) -> p i r u", i=count, u=2),
+                in_=d_bank[batch][:, :count, :, :].rearrange("p i u r -> p i r u"),
             )
 
+        def turn_and_gather(some):
+            for batch in some:
+                turn(batch)
+                gather(batch)
+
         def quantize_d(some):
-            cells = [unit for batch in some for unit in batch]
-            g, t, c = cells[0]
-            name = "%d_%d_%d" % cells[0]
-            codes = keep.tile([P, len(cells) * P], U32, name="d_codes_" + name, align_bytes=64)
-            scales = keep.tile([P, len(cells) * P], U8, name="d_scales_" + name, align_bytes=64)
+            joined = [cell for batch in some for cell in batch]
+            g, t, c = joined[0]
+            name = "%d_%d_%d" % joined[0]
+            codes = keep.tile([P, len(joined) * P], U32, name="d_codes_" + name, align_bytes=64)
+            scales = keep.tile([P, len(joined) * P], U8, name="d_scales_" + name, align_bytes=64)
             at = (t * PASSES + c) * SPAN
-            grouped = d_stage[g][:, at:at + len(cells) * SPAN]
+            grouped = d_stage[g][:, at:at + len(joined) * SPAN]
             nc.vector.quantize_mx(out=codes[:].bitcast(E4M3X4), scales=scales[:], in_=grouped)
-            for i, unit in enumerate(cells):
-                d_codes[unit] = codes[:, i * P:(i + 1) * P]
-                d_scales[unit] = scales[:, i * P:(i + 1) * P]
+            for i, cell in enumerate(joined):
+                d_codes[cell] = codes[:, i * P:(i + 1) * P]
+                d_scales[cell] = scales[:, i * P:(i + 1) * P]
 
         last = GROUPS - 1
         y_wide = [keep.tile([P, PACK, RHS], F32, name="y_f32_%d" % g) for g in range(last)]
-        y_half = [keep.tile([P, PACK, N], F32, name="y_f32_last_%d" % h) for h in range(HALVES)]
+        y_half = [keep.tile([P, PACK, N], F32, name="y_f32_last_%d" % h) for h in range(RHS // N)]
         y_bf16 = [keep.tile([P, RHS, PACK], BF16, name="y_bf16_%d" % g, align_bytes=64) for g in range(GROUPS)]
         y_codes = [keep.tile([P, RHS], U32, name="y_codes_%d" % g, align_bytes=64) for g in range(GROUPS)]
         y_plane = keep.tile([P, GROUPS, RHS], U8, name="y_plane", align_bytes=64)
@@ -218,33 +240,48 @@ def tile_schur_closing_hop_k2_kernel(tc, d_eo, chi_words, chi_scales, phi, kappa
                     out=bank[:],
                     lhsT=d_codes[(g, t, c)].bitcast(E4M3X4),
                     lhsT_scale=d_scales[(g, t, c)],
-                    rhs=chi_sb[(h, c)].bitcast(E5M2X4),
+                    rhs=chi_codes[(h, c)].bitcast(E5M2X4),
                     rhs_scale=chi_plane[:, c * RHS + h * N:c * RHS + (h + 1) * N],
                     start=(c == 0),
                     stop=(c == PASSES - 1),
                 )
             hop[(g, t, h)] = bank
 
-        def scale(g, t, h, n0, n1):
-            r0, r1 = h * N + n0, h * N + n1
+        def scale(g, t, r0, r1):
+            h = r0 // N
             nc.vector.tensor_tensor(
-                out=y_f32(g, t, t + 1, r0, r1)[:, 0, :], in0=hop[(g, t, h)][:, n0:n1], in1=kappa2_row[:, r0:r1], op=ALU.mult
+                out=y_f32(g, t, t + 1, r0, r1)[:, 0, :],
+                in0=kappa2_row[:, r0:r1],
+                in1=hop[(g, t, h)][:, r0 - h * N:r1 - h * N],
+                op=ALU.mult,
             )
+
+        def product(g, t, h):
+            multiply(g, t, h)
+            scale(g, t, h * N, (h + 1) * N)
 
         def subtract(engine, g, t0, t1, r0, r1):
             part = y_f32(g, t0, t1, r0, r1)
-            rows, at = phi_sb[(g, t0)]
+            rows, at = phi_rows[(g, t0)]
             engine.tensor_tensor(out=part, in0=rows[:, at:at + t1 - t0, r0:r1], in1=part, op=ALU.subtract)
 
-        def subtract_rest(engine, g, pair):
-            part = y_f32(g, 2 * pair, 2 * pair + 2, 0, RHS).rearrange("p t r -> p (t r)")[:, N:]
-            rows = phi_sb[(g, 2 * pair)][0][:].rearrange("p t r -> p (t r)")[:, N:]
-            engine.tensor_tensor(out=part, in0=rows, in1=part, op=ALU.subtract)
+        def subtract_rest(g, t):
+            part = y_f32(g, t, t + 2, 0, RHS).rearrange("p t r -> p (t r)")[:, N:]
+            rows = phi_rows[(g, t)][0][:].rearrange("p t r -> p (t r)")[:, N:]
+            nc.vector.tensor_tensor(out=part, in0=rows, in1=part, op=ALU.subtract)
+
+        def lead_product(g, t, h):
+            product(g, t, h)
+            subtract(gpsimd, g, t, t + 1, h * N, (h + 1) * N)
 
         def weave(engine, g, r0, r1):
             dst = y_bf16[g][:, r0:r1, :].rearrange("p (c i) t -> p c t i", i=4)
             src = y_f32(g, 0, PACK, r0, r1).rearrange("p t (c i) -> p c t i", i=4)
             copy_on(engine, dst, src)
+
+        def weave_quarters(g, r0, r1):
+            for r in range(r0, r1, QUARTER):
+                weave(scalar, g, r, r + QUARTER)
 
         def quantize_y(g, r0, r1):
             nc.vector.quantize_mx(
@@ -262,196 +299,110 @@ def tile_schur_closing_hop_k2_kernel(tc, d_eo, chi_words, chi_scales, phi, kappa
             nc.sync.dma_start(out=dst.bitcast(I32), in_=y_codes[g][:, r0:r1].bitcast(I32))
 
         def store_plane(g0, g1, queues):
-            for q in range(4):
+            for q in range(QUADRANTS):
                 queues[q % len(queues)].dma_start(
                     out=out_2[g0:g1, 4 * q:4 * q + 4, :].rearrange("g q n -> q g n").bitcast(I32),
                     in_=y_plane[32 * q:32 * q + 4, g0:g1, :].bitcast(I32),
                 )
 
-        load_d(0, 0, 1)
-        load_d(0, 1, 2)
-        load_kappa()
-        load_chi(0, 1, 3)
-        warm()
-        load_chi_scales()
-        warm()
-        warm()
-        load_chi(0, 0, 1)
-        split_words(vector, work[0][0])
-        warm()
-        load_d(0, 2, 3)
-        split_words(scalar, work[0][2])
-        load_d(0, 3, 4)
-        turn(work[0][0])
-        square_kappa()
-        split_words(vector, work[0][3])
+
+        warm(4)
+        split_words(vector, slot0[0])
+        nc.vector.tensor_tensor(out=kappa2_col[:], in0=kappa_sb[:], in1=kappa_sb[:], op=ALU.mult)
+        split_words(vector, slot0[1])
+        split_words(vector, slot1[0])
+        split_words(scalar, slot1[1])
+        turn_and_gather([slot0[1], slot0[0]])
+        warm(3)
         spread_kappa2(0)
-        split_words(scalar, work[0][1])
-        turn(work[0][3])
-        gather(work[0][0])
-        turn(work[0][2])
-        load_chi(1, 0, 3)
-        spread_kappa2(1)
-        gather(work[0][2])
-        quantize_d([work[0][0]])
-        turn(work[0][1])
-        warm()
-        load_phi(0, 0, 2)
-        load_d(1, 0, 2)
-        gather(work[0][1])
-        warm()
-        load_phi(0, 2, 4)
-        load_d(1, 2, 4)
-        warm()
+        turn_and_gather([slot1[0]])
         copy_kappa2(0)
-        quantize_d([work[0][1]])
-        load_d(2, 2, 4)
-        multiply(0, 0, 0)
-        gather(work[0][3])
+        spread_kappa2(1)
+        turn_and_gather([slot1[1]])
         copy_kappa2(1)
-        load_phi(1, 0, 2)
-        quantize_d([work[0][3]])
-        turn(work[0][6])
-        quantize_d([work[0][2]])
-        turn(work[0][7])
-        load_phi(1, 2, 4)
-        split_words(vector, work[0][8])
-        gather(work[0][6])
-        scale(0, 0, 0, 0, 512)
-        turn(work[0][8])
-        gather(work[0][7])
-        multiply(0, 1, 0)
-        gather(work[0][8])
-        quantize_d(work[0][6:8])
-        load_d(2, 0, 2)
-        multiply(0, 0, 1)
-        quantize_d([work[0][8]])
-        scale(0, 1, 0, 0, 512)
-        multiply(0, 1, 1)
-        load_phi(2, 0, 4)
-        subtract(gpsimd, 0, 0, 1, 0, 512)
-        scale(0, 0, 1, 0, 512)
-        multiply(0, 2, 0)
-        scale(0, 1, 1, 0, 512)
-        multiply(0, 3, 0)
-        split_words(scalar, work[1][1])
-        subtract(vector, 0, 1, 2, 0, 512)
-        split_words(scalar, work[1][0])
-        scale(0, 2, 0, 0, 512)
-        multiply(0, 2, 1)
-        split_words(scalar, work[1][2])
-        subtract(vector, 0, 0, 2, 512, 1024)
-        turn(work[1][0])
-        turn(work[1][1])
-        subtract(gpsimd, 0, 2, 3, 0, 512)
-        scale(0, 3, 0, 0, 512)
-        gather(work[1][0])
-        multiply(0, 3, 1)
-        gather(work[1][1])
-        scale(0, 2, 1, 0, 512)
-        turn(work[1][2])
-        split_words(scalar, work[1][5])
-        scale(0, 3, 1, 0, 512)
-        turn(work[1][4])
-        gather(work[1][2])
-        quantize_d(work[1][0:2])
-        turn(work[1][3])
-        gather(work[1][4])
-        turn(work[1][5])
-        subtract_rest(vector, 0, 1)
-        multiply(1, 0, 0)
-        gather(work[1][3])
-        split_words(scalar, work[2][3])
-        multiply(1, 0, 1)
-        gather(work[1][5])
-        quantize_d(work[1][2:4])
-        store_y(0, 2, 4, 0, RHS)
+        for batch in slot0 + slot1[:1]:
+            quantize_d([batch])
+        split_words(vector, slots23[2])
+        lead_product(0, 0, 0)
+        turn_and_gather(slots23)
+        quantize_d(slot1[1:])
+        quantize_d(slots23[:2])
+        quantize_d(slots23[2:])
+        product(0, 1, 0)
+        product(0, 0, 1)
+        product(0, 1, 1)
+        subtract(vector, 0, 1, 2, 0, N)
+
+        lead_product(0, 2, 0)
+        subtract(vector, 0, 0, 2, N, RHS)
         store_y(0, 0, 2, 0, RHS)
-        multiply(1, 1, 0)
-        weave(scalar, 0, 0, 256)
-        scale(1, 0, 0, 0, 512)
-        scale(1, 0, 1, 0, 512)
-        multiply(1, 1, 1)
-        subtract(gpsimd, 1, 0, 1, 0, 512)
-        weave(scalar, 0, 512, 768)
-        scale(1, 1, 0, 0, 512)
-        turn(work[2][1])
-        scale(1, 1, 1, 0, 512)
-        turn(work[2][0])
-        weave(scalar, 0, 768, 1024)
-        quantize_d(work[1][4:6])
-        multiply(1, 2, 0)
-        subtract_rest(vector, 1, 0)
-        split_words(scalar, work[2][4])
-        multiply(1, 2, 1)
-        gather(work[2][1])
-        multiply(1, 3, 0)
-        scale(1, 2, 0, 0, 512)
-        weave(scalar, 0, 256, 512)
+        product(0, 2, 1)
+        product(0, 3, 0)
+        for batch in batches[1][:2]:
+            split_words(scalar, batch)
+        turn_and_gather(batches[1][:2])
+        product(0, 3, 1)
+        turn_and_gather(batches[1][2:])
+        for batch in batches[2][:2]:
+            split_words(scalar, batch)
+        quantize_d(batches[1][0:2])
+        subtract_rest(0, 2)
+        store_y(0, 2, 4, 0, RHS)
+        weave_quarters(0, 0, RHS - QUARTER)
+        quantize_d(batches[1][2:4])
+
+        lead_product(1, 0, 0)
+        quantize_d(batches[1][4:6])
+        product(1, 0, 1)
+        product(1, 1, 0)
+        product(1, 1, 1)
+
+        lead_product(1, 2, 0)
+        subtract_rest(1, 0)
         store_y(1, 0, 2, 0, RHS)
-        scale(1, 2, 1, 0, 512)
-        multiply(1, 3, 1)
-        subtract(gpsimd, 1, 2, 3, 0, 512)
-        scale(1, 3, 0, 0, 512)
-        gather(work[2][0])
-        turn(work[2][3])
-        scale(1, 3, 1, 0, 512)
-        turn(work[2][2])
-        gather(work[2][3])
-        turn(work[2][4])
-        quantize_d(work[2][0:2])
-        gather(work[2][2])
-        turn(work[2][5])
-        subtract_rest(vector, 1, 1)
-        multiply(2, 0, 0)
-        gather(work[2][5])
-        gather(work[2][4])
-        quantize_d(work[2][2:4])
-        multiply(2, 1, 0)
+        product(1, 2, 1)
+        turn_and_gather(batches[2][:2])
+        weave_quarters(0, RHS - QUARTER, RHS)
+        product(1, 3, 0)
+        product(1, 3, 1)
+        turn_and_gather(batches[2][2:])
+        quantize_d(batches[2][0:2])
+        subtract_rest(1, 2)
         store_y(1, 2, 4, 0, RHS)
-        weave(scalar, 1, 256, 512)
-        quantize_d(work[2][4:6])
-        quantize_y(0, 0, 1024)
-        multiply(2, 3, 0)
-        weave(scalar, 1, 512, 768)
-        multiply(2, 3, 1)
-        scale(2, 0, 0, 0, 512)
+        weave_quarters(1, 0, RHS)
+        quantize_d(batches[2][2:4])
+        quantize_d(batches[2][4:6])
+
+        middle = N + QUARTER
+        lead_product(last, 0, 0)
+        quantize_y(0, 0, RHS)
         store_codes(0, 0, RHS)
-        weave(scalar, 1, 0, 256)
-        scale(2, 1, 0, 0, 512)
-        multiply(2, 2, 0)
-        subtract(gpsimd, 2, 0, 1, 0, 512)
-        scale(2, 3, 0, 0, 512)
-        multiply(2, 1, 1)
-        weave(scalar, 1, 768, 1024)
-        scale(2, 2, 0, 0, 512)
-        multiply(2, 2, 1)
-        scale(2, 3, 1, 0, 256)
-        subtract(vector, 2, 1, 4, 0, 512)
-        multiply(2, 0, 1)
-        scale(2, 0, 1, 0, 512)
-        weave(scalar, 2, 0, 256)
-        store_y(2, 0, 4, 0, 512)
-        quantize_y(1, 0, 1024)
-        weave(scalar, 2, 256, 512)
-        subtract(gpsimd, 2, 0, 1, 512, 1024)
-        scale(2, 2, 1, 0, 512)
+        for t in range(1, PACK):
+            product(last, t, 0)
+        multiply(last, 3, 1)
+        scale(last, 3, N, middle)
+        subtract(vector, last, 1, PACK, 0, N)
+        store_y(last, 0, PACK, 0, N)
+        weave_quarters(last, 0, N)
+
+        lead_product(last, 0, 1)
+        quantize_y(1, 0, RHS)
         store_codes(1, 0, RHS)
-        scale(2, 3, 1, 256, 512)
-        scale(2, 1, 1, 0, 512)
-        store_y(2, 0, 1, 512, 1024)
-        store_plane(0, 2, [nc.sync])
-        subtract(vector, 2, 3, 4, 512, 768)
-        subtract(vector, 2, 1, 3, 512, 1024)
-        subtract(vector, 2, 3, 4, 768, 1024)
-        weave(scalar, 2, 512, 768)
-        store_y(2, 1, 3, 512, 1024)
-        store_y(2, 3, 4, 512, 1024)
-        weave(vector, 2, 896, 1024)
-        quantize_y(2, 0, 512)
-        weave(scalar, 2, 768, 896)
-        quantize_y(2, 512, 768)
-        store_codes(2, 0, 512)
-        quantize_y(2, 768, 1024)
-        store_codes(2, 512, 1024)
-        store_plane(2, 3, [nc.sync, nc.scalar])
+        store_plane(0, last, [nc.sync])
+        store_y(last, 0, 1, N, RHS)
+        scale(last, 3, middle, RHS)
+        product(last, 1, 1)
+        product(last, 2, 1)
+        subtract(vector, last, 3, 4, N, middle)
+        subtract(vector, last, 1, 3, N, RHS)
+        store_y(last, 1, 3, N, RHS)
+        weave(scalar, last, N, middle)
+        subtract(vector, last, 3, 4, middle, RHS)
+        store_y(last, 3, 4, N, RHS)
+        quantize_y(last, 0, N)
+        store_codes(last, 0, N)
+        weave(vector, last, middle, RHS)
+        quantize_y(last, N, middle)
+        quantize_y(last, middle, RHS)
+        store_codes(last, N, RHS)
+        store_plane(last, GROUPS, [nc.sync, nc.scalar])

from contextlib import ExitStack

import concourse.mybir as mybir
from concourse.masks import make_identity

EVEN, ODD, RHS = 1536, 1536, 1024
FLOPS = 2 * EVEN * ODD * RHS

F32 = mybir.dt.float32
BF16 = mybir.dt.bfloat16
I32 = mybir.dt.int32
U32 = mybir.dt.uint32
U8 = mybir.dt.uint8
E4M3X4 = mybir.dt.float8_e4m3fn_x4
E5M2X4 = mybir.dt.float8_e5m2_x4
ALU = mybir.AluOpType

P = 128
PACK = 4
SPAN = P * PACK
GROUPS = EVEN // SPAN
PASSES = ODD // SPAN
N = 512
QUARTER = N // 2
PAIRS = SPAN // 2
QUADRANTS = 4

TURN_BANKS = 3
HOP_BANKS = 5
SPLIT_TILES = 5
STAGE_TILES = 2


def tile_schur_closing_hop_k2_kernel(tc, d_eo, chi_words, chi_scales, phi, kappa, out_0, out_1, out_2):
    nc = tc.nc
    vector, scalar, gpsimd = nc.vector, nc.scalar, nc.gpsimd
    with ExitStack() as ctx:
        keep = ctx.enter_context(tc.tile_pool(name="keep", bufs=1))
        psum = ctx.enter_context(tc.psum_pool(name="psum", bufs=1))
        ctx.enter_context(tc.manual_schedule())

        turn_tiles = []
        hop_tiles = []

        def turn_tile():
            bank = psum.tile([P, 2, 2, P], F32, name="turn_bank_%d" % (len(turn_tiles) % TURN_BANKS))
            turn_tiles.append(bank)
            return bank

        def hop_tile():
            bank = psum.tile([P, N], F32, name="hop_bank_%d" % (len(hop_tiles) % HOP_BANKS))
            hop_tiles.append(bank)
            return bank

        def copy_on(engine, out, in_):
            if engine is scalar:
                nc.scalar.copy(out=out, in_=in_)
            else:
                nc.vector.tensor_copy(out=out, in_=in_)

        zeros = keep.tile([P, SPAN], BF16, name="zeros", align_bytes=64)
        nc.vector.memset(zeros[:].bitcast(I32), 0)
        warm_codes = keep.tile([P, N + P], U32, name="warm_codes", align_bytes=64)
        warm_scales = keep.tile([P, N + P], U8, name="warm_scales", align_bytes=64)
        for n0 in range(0, N, P):
            cols = slice(n0, n0 + P)
            nc.vector.quantize_mx(out=warm_codes[:, cols].bitcast(E5M2X4), scales=warm_scales[:, cols], in_=zeros[:])
        nc.vector.quantize_mx(out=warm_codes[:, N:].bitcast(E4M3X4), scales=warm_scales[:, N:], in_=zeros[:])
        warm_bank = hop_tile()

        def warm(count):
            for repeat in range(count):
                nc.tensor.matmul_mx(
                    out=warm_bank[:],
                    lhsT=warm_codes[:, N:].bitcast(E4M3X4),
                    lhsT_scale=warm_scales[:, N:],
                    rhs=warm_codes[:, :N].bitcast(E5M2X4),
                    rhs_scale=warm_scales[:, :N],
                    start=True,
                    stop=True,
                )

        chi_plane = keep.tile([P, PASSES * RHS], U8, name="chi_plane", align_bytes=64)
        nc.vector.memset(chi_plane[:].bitcast(I32), 0)
        ident = keep.tile([P, P], F32, name="ident")
        nc.vector.memset(ident[:], 0.0)
        make_identity(nc, ident[:], nomemset=True)

        d_words = {}
        phi_rows = {}
        chi_codes = {}
        kappa_sb = keep.tile([P, RHS // P], BF16, name="kappa_sb")

        def load_d(g, t0, t1):
            raw = keep.tile([P, t1 - t0, ODD], BF16, name="d_raw_%d_%d" % (g, t0))
            src = d_eo[g * SPAN:(g + 1) * SPAN, :].rearrange("(p t) k -> p t k", t=PACK)
            nc.sync.dma_start(out=raw[:], in_=src[:, t0:t1, :])
            for t in range(t0, t1):
                d_words[(g, t)] = raw[:, t - t0, :].bitcast(F32)

        def load_phi(g, t0, t1):
            raw = keep.tile([P, t1 - t0, RHS], BF16, name="phi_%d_%d" % (g, t0))
            src = phi[g * SPAN:(g + 1) * SPAN, :].rearrange("(p t) r -> p t r", t=PACK)
            nc.sync.dma_start(out=raw[:], in_=src[:, t0:t1, :])
            for t in range(t0, t1):
                phi_rows[(g, t)] = (raw, t - t0)

        def load_chi(h, c0, c1):
            raw = keep.tile([P, c1 - c0, N], U32, name="chi_%d_%d" % (h, c0), align_bytes=64)
            src = chi_words.rearrange("c p n i -> p c (n i)")[:, c0:c1, h * N * PACK:(h + 1) * N * PACK]
            nc.sync.dma_start(out=raw[:].bitcast(I32), in_=src.bitcast(I32))
            for c in range(c0, c1):
                chi_codes[(h, c)] = raw[:, c - c0, :]

        load_d(0, 0, 1)
        nc.sync.dma_start(
            out=kappa_sb[:].rearrange("p (h m) -> p h m", m=PACK),
            in_=kappa.rearrange("(h p m) -> p h m", p=P, m=PACK),
        )
        load_d(0, 1, 2)
        load_chi(0, 0, 1)
        for q in range(QUADRANTS):
            nc.sync.dma_start(
                out=chi_plane[32 * q:32 * q + 4, :].rearrange("p (c n) -> p c n", c=PASSES).bitcast(I32),
                in_=chi_scales[:, 4 * q:4 * q + 4, :].rearrange("c q n -> q c n").bitcast(I32),
            )
        load_chi(0, 1, PASSES)
        load_d(0, 2, 3)
        load_d(0, 3, 4)
        load_chi(1, 0, PASSES)
        load_phi(0, 0, 2)
        load_d(1, 0, 2)
        load_phi(0, 2, 4)
        load_d(1, 2, 4)
        load_phi(1, 0, 2)
        load_phi(1, 2, 4)
        load_d(2, 0, 2)
        load_d(2, 2, 4)
        load_phi(2, 0, 4)

        kappa2_col = keep.tile([P, RHS // P], F32, name="kappa2_col")
        kappa2_row = keep.tile([P, RHS], F32, name="kappa2_row")
        kappa2_bank = {}

        def spread_kappa2(h):
            bank = hop_tile()
            for m in range(PACK):
                column = kappa2_col[:, h * PACK + m:h * PACK + m + 1]
                nc.tensor.transpose(bank[:, m * P:(m + 1) * P], column.to_broadcast([P, P]), ident[:])
            kappa2_bank[h] = bank

        def copy_kappa2(h):
            nc.scalar.copy(
                out=kappa2_row[:, h * N:(h + 1) * N].rearrange("p (j m) -> p j m", m=PACK),
                in_=kappa2_bank[h][:].rearrange("p (m j) -> p j m", m=PACK),
            )

        cells = [[(g, t, c) for t in range(PACK) for c in range(PASSES)] for g in range(GROUPS)]
        batches = [[tuple(row[i:i + 2]) for i in range(0, len(row), 2)] for row in cells]
        slot0 = [tuple(cells[0][0:2]), tuple(cells[0][2:3])]
        slot1 = [tuple(cells[0][3:5]), tuple(cells[0][5:6])]
        slots23 = batches[0][3:]
        d_split = {}
        d_bank = {}
        d_stage = {}
        d_codes = {}
        d_scales = {}

        def split_words(engine, batch):
            g, t, c = batch[0]
            count = len(batch)
            split = keep.tile([P, count, 2, P], F32, name="d_split", bufs=SPLIT_TILES)
            if batch[-1][1] == t:
                src = d_words[(g, t)][:, PAIRS * c:PAIRS * (c + count)]
                copy_on(engine, split[:], src.rearrange("p (i w u) -> p i u w", i=count, u=2))
            else:
                for i, (g, t, c) in enumerate(batch):
                    src = d_words[(g, t)][:, PAIRS * c:PAIRS * (c + 1)]
                    copy_on(engine, split[:, i, :, :], src.rearrange("p (w u) -> p u w", u=2))
            d_split[batch] = split

        def turn(batch):
            bank = turn_tile()
            for i, (g, t, c) in enumerate(batch):
                for u in range(2):
                    if batch in d_split:
                        words = d_split[batch][:, i, u, :]
                    else:
                        words = d_words[(g, t)][:, PAIRS * c + u:PAIRS * (c + 1):2]
                    nc.tensor.transpose(bank[:, i, u, :], words, ident[:])
            d_bank[batch] = bank

        def gather(batch):
            count = len(batch)
            g, t, c = batch[0]
            if g not in d_stage:
                d_stage[g] = keep.tile([P, PACK * ODD], BF16, name="d_grouped", bufs=STAGE_TILES, align_bytes=64)
            at = (t * PASSES + c) * SPAN
            nc.scalar.copy(
                out=d_stage[g][:, at:at + count * SPAN].bitcast(F32).rearrange("p (i r u) -> p i r u", i=count, u=2),
                in_=d_bank[batch][:, :count, :, :].rearrange("p i u r -> p i r u"),
            )

        def turn_and_gather(some):
            for batch in some:
                turn(batch)
                gather(batch)

        def quantize_d(some):
            joined = [cell for batch in some for cell in batch]
            g, t, c = joined[0]
            name = "%d_%d_%d" % joined[0]
            codes = keep.tile([P, len(joined) * P], U32, name="d_codes_" + name, align_bytes=64)
            scales = keep.tile([P, len(joined) * P], U8, name="d_scales_" + name, align_bytes=64)
            at = (t * PASSES + c) * SPAN
            grouped = d_stage[g][:, at:at + len(joined) * SPAN]
            nc.vector.quantize_mx(out=codes[:].bitcast(E4M3X4), scales=scales[:], in_=grouped)
            for i, cell in enumerate(joined):
                d_codes[cell] = codes[:, i * P:(i + 1) * P]
                d_scales[cell] = scales[:, i * P:(i + 1) * P]

        last = GROUPS - 1
        y_wide = [keep.tile([P, PACK, RHS], F32, name="y_f32_%d" % g) for g in range(last)]
        y_half = [keep.tile([P, PACK, N], F32, name="y_f32_last_%d" % h) for h in range(RHS // N)]
        y_bf16 = [keep.tile([P, RHS, PACK], BF16, name="y_bf16_%d" % g, align_bytes=64) for g in range(GROUPS)]
        y_codes = [keep.tile([P, RHS], U32, name="y_codes_%d" % g, align_bytes=64) for g in range(GROUPS)]
        y_plane = keep.tile([P, GROUPS, RHS], U8, name="y_plane", align_bytes=64)
        hop = {}

        def y_f32(g, t0, t1, r0, r1):
            if g < last:
                return y_wide[g][:, t0:t1, r0:r1]
            h = r0 // N
            return y_half[h][:, t0:t1, r0 - h * N:r1 - h * N]

        def multiply(g, t, h):
            bank = hop_tile()
            for c in range(PASSES):
                nc.tensor.matmul_mx(
                    out=bank[:],
                    lhsT=d_codes[(g, t, c)].bitcast(E4M3X4),
                    lhsT_scale=d_scales[(g, t, c)],
                    rhs=chi_codes[(h, c)].bitcast(E5M2X4),
                    rhs_scale=chi_plane[:, c * RHS + h * N:c * RHS + (h + 1) * N],
                    start=(c == 0),
                    stop=(c == PASSES - 1),
                )
            hop[(g, t, h)] = bank

        def scale(g, t, r0, r1):
            h = r0 // N
            nc.vector.tensor_tensor(
                out=y_f32(g, t, t + 1, r0, r1)[:, 0, :],
                in0=kappa2_row[:, r0:r1],
                in1=hop[(g, t, h)][:, r0 - h * N:r1 - h * N],
                op=ALU.mult,
            )

        def product(g, t, h):
            multiply(g, t, h)
            scale(g, t, h * N, (h + 1) * N)

        def subtract(engine, g, t0, t1, r0, r1):
            part = y_f32(g, t0, t1, r0, r1)
            rows, at = phi_rows[(g, t0)]
            engine.tensor_tensor(out=part, in0=rows[:, at:at + t1 - t0, r0:r1], in1=part, op=ALU.subtract)

        def subtract_rest(g, t):
            part = y_f32(g, t, t + 2, 0, RHS).rearrange("p t r -> p (t r)")[:, N:]
            rows = phi_rows[(g, t)][0][:].rearrange("p t r -> p (t r)")[:, N:]
            nc.vector.tensor_tensor(out=part, in0=rows, in1=part, op=ALU.subtract)

        def lead_product(g, t, h):
            product(g, t, h)
            subtract(gpsimd, g, t, t + 1, h * N, (h + 1) * N)

        def weave(engine, g, r0, r1):
            dst = y_bf16[g][:, r0:r1, :].rearrange("p (c i) t -> p c t i", i=4)
            src = y_f32(g, 0, PACK, r0, r1).rearrange("p t (c i) -> p c t i", i=4)
            copy_on(engine, dst, src)

        def weave_quarters(g, r0, r1):
            for r in range(r0, r1, QUARTER):
                weave(scalar, g, r, r + QUARTER)

        def quantize_y(g, r0, r1):
            nc.vector.quantize_mx(
                out=y_codes[g][:, r0:r1].bitcast(E4M3X4),
                scales=y_plane[:, g, r0:r1],
                in_=y_bf16[g][:, r0:r1, :].rearrange("p n t -> p (n t)"),
            )

        def store_y(g, t0, t1, r0, r1):
            dst = out_0[g * SPAN:(g + 1) * SPAN, r0:r1].rearrange("(p t) r -> p t r", t=PACK)
            nc.sync.dma_start(out=dst[:, t0:t1, :], in_=y_f32(g, t0, t1, r0, r1))

        def store_codes(g, r0, r1):
            dst = out_1[g].rearrange("p n t -> p (n t)")[:, r0 * PACK:r1 * PACK]
            nc.sync.dma_start(out=dst.bitcast(I32), in_=y_codes[g][:, r0:r1].bitcast(I32))

        def store_plane(g0, g1, queues):
            for q in range(QUADRANTS):
                queues[q % len(queues)].dma_start(
                    out=out_2[g0:g1, 4 * q:4 * q + 4, :].rearrange("g q n -> q g n").bitcast(I32),
                    in_=y_plane[32 * q:32 * q + 4, g0:g1, :].bitcast(I32),
                )


        warm(4)
        split_words(vector, slot0[0])
        nc.vector.tensor_tensor(out=kappa2_col[:], in0=kappa_sb[:], in1=kappa_sb[:], op=ALU.mult)
        split_words(vector, slot0[1])
        split_words(vector, slot1[0])
        split_words(scalar, slot1[1])
        turn_and_gather([slot0[1], slot0[0]])
        warm(3)
        spread_kappa2(0)
        turn_and_gather([slot1[0]])
        copy_kappa2(0)
        spread_kappa2(1)
        turn_and_gather([slot1[1]])
        copy_kappa2(1)
        for batch in slot0 + slot1[:1]:
            quantize_d([batch])
        split_words(vector, slots23[2])
        lead_product(0, 0, 0)
        turn_and_gather(slots23)
        quantize_d(slot1[1:])
        quantize_d(slots23[:2])
        quantize_d(slots23[2:])
        product(0, 1, 0)
        product(0, 0, 1)
        product(0, 1, 1)
        subtract(vector, 0, 1, 2, 0, N)

        lead_product(0, 2, 0)
        subtract(vector, 0, 0, 2, N, RHS)
        store_y(0, 0, 2, 0, RHS)
        product(0, 2, 1)
        product(0, 3, 0)
        for batch in batches[1][:2]:
            split_words(scalar, batch)
        turn_and_gather(batches[1][:2])
        product(0, 3, 1)
        turn_and_gather(batches[1][2:])
        for batch in batches[2][:2]:
            split_words(scalar, batch)
        quantize_d(batches[1][0:2])
        subtract_rest(0, 2)
        store_y(0, 2, 4, 0, RHS)
        weave_quarters(0, 0, RHS - QUARTER)
        quantize_d(batches[1][2:4])

        lead_product(1, 0, 0)
        quantize_d(batches[1][4:6])
        product(1, 0, 1)
        product(1, 1, 0)
        product(1, 1, 1)

        lead_product(1, 2, 0)
        subtract_rest(1, 0)
        store_y(1, 0, 2, 0, RHS)
        product(1, 2, 1)
        turn_and_gather(batches[2][:2])
        weave_quarters(0, RHS - QUARTER, RHS)
        product(1, 3, 0)
        product(1, 3, 1)
        turn_and_gather(batches[2][2:])
        quantize_d(batches[2][0:2])
        subtract_rest(1, 2)
        store_y(1, 2, 4, 0, RHS)
        weave_quarters(1, 0, RHS)
        quantize_d(batches[2][2:4])
        quantize_d(batches[2][4:6])

        middle = N + QUARTER
        lead_product(last, 0, 0)
        quantize_y(0, 0, RHS)
        store_codes(0, 0, RHS)
        for t in range(1, PACK):
            product(last, t, 0)
        multiply(last, 3, 1)
        scale(last, 3, N, middle)
        subtract(vector, last, 1, PACK, 0, N)
        store_y(last, 0, PACK, 0, N)
        weave_quarters(last, 0, N)

        lead_product(last, 0, 1)
        quantize_y(1, 0, RHS)
        store_codes(1, 0, RHS)
        store_plane(0, last, [nc.sync])
        store_y(last, 0, 1, N, RHS)
        scale(last, 3, middle, RHS)
        product(last, 1, 1)
        product(last, 2, 1)
        subtract(vector, last, 3, 4, N, middle)
        subtract(vector, last, 1, 3, N, RHS)
        store_y(last, 1, 3, N, RHS)
        weave(scalar, last, N, middle)
        subtract(vector, last, 3, 4, middle, RHS)
        store_y(last, 3, 4, N, RHS)
        quantize_y(last, 0, N)
        store_codes(last, 0, N)
        weave(vector, last, middle, RHS)
        quantize_y(last, N, middle)
        quantize_y(last, middle, RHS)
        store_codes(last, N, RHS)
        store_plane(last, GROUPS, [nc.sync, nc.scalar])
